import numpy as np
import ml_dtypes


def mxq(x, axis, fmt="e4m3"):
    dtype, down = {"e4m3": (ml_dtypes.float8_e4m3fn, 7), "e5m2": (ml_dtypes.float8_e5m2, 14)}[fmt]
    v = np.moveaxis(np.asarray(x, np.float32).astype(ml_dtypes.bfloat16).astype(np.float64), axis, -1)
    blocks = v.reshape(v.shape[:-1] + (-1, 32))
    amax = np.abs(blocks).max(-1, keepdims=True)
    byte = np.maximum(np.where(amax > 0, np.frexp(amax)[1] - 1 + 127, 0) - down, 1)
    scale = np.exp2(byte - 127.0)
    codes = (blocks / scale).astype(np.float32).astype(dtype).astype(np.float64)
    return np.moveaxis((codes * scale).reshape(v.shape), -1, axis)


WIDE = False


def mx_kscale(k):
    if not WIDE:
        return np.ones(k)
    levels = np.array([10, -10, 5, -5, 0])
    if k % 512:
        return np.exp2(np.random.permutation(np.resize(levels, k // 32))).repeat(32)
    a = np.empty((k // 512, 16))
    for p in range(k // 512):
        a[p, :8] = np.random.permutation(np.resize(levels, 8))
        for g in range(8):
            far = levels[np.abs(levels - a[p, g]) >= 10]
            a[p, g + 8] = far[np.random.randint(len(far))]
    return np.exp2(a.ravel()).repeat(32)


def f64(x):
    return np.asarray(x).astype(np.float64)


def striped(idx):
    return np.tile(idx.reshape(-1, 16).T, (8, 1)).astype(np.uint16)


def unstriped(offs):
    return offs[:16].T.reshape(-1).astype(np.int64)

def planes(y):
    n, m = y.shape
    v = y.astype(np.float32).astype(ml_dtypes.bfloat16).astype(np.float64).reshape(n // 32, 32, m)
    top = np.abs(v).max(1)
    byte = np.clip(np.where(top > 0, np.frexp(top)[1] - 1 + 127 - 7, 1), 1, 254)
    codes = (v * np.exp2(127.0 - byte)[:, None, :]).reshape(n, m).astype(np.float32).astype(ml_dtypes.float8_e4m3fn).view(np.uint8)
    words = codes.reshape(n // 512, 128, 4, m).transpose(0, 1, 3, 2)
    return np.ascontiguousarray(words), np.ascontiguousarray(byte.astype(np.uint8).reshape(n // 512, 16, m))


K, T, S, V, N = 512, 1024, 512, 256, 512


def setup_inputs():
    n = np.random.standard_normal
    s = mx_kscale(K)[:, None]
    return {
        "xT": (n((K, T)) * s).astype(np.float32),
        "w1": (n((K, N)) / np.sqrt(K) / s).astype(np.float32),
        "offs": striped(np.random.permutation(T)[:S]),
        "pos1": striped(np.random.permutation(S)[:V]),
        "pos2": striped(np.random.permutation(S)[:V]),
        "pos3": striped(np.random.permutation(S)[:V]),
    }


def reference(xT, w1, offs, pos1, pos2, pos3):
    xq = mxq(f64(xT)[:, unstriped(offs)], 0, "e4m3")
    y = mxq(f64(w1), 0, "e4m3").T @ xq
    n0 = y[:, unstriped(pos1)]
    n1 = y[:, unstriped(pos2)]
    n2 = y[:, unstriped(pos3)]
    out_0 = np.maximum(np.minimum(n0, n1), np.minimum(np.maximum(n0, n1), n2))
    return (out_0,) + planes(out_0)

@@ -1,0 +1,173 @@
+from contextlib import ExitStack
+
+import concourse.mybir as mybir
+
+K, T, S, V, N = 512, 1024, 512, 256, 512
+FLOPS = 2 * K * N * S
+
+F32 = mybir.dt.float32
+BF16 = mybir.dt.bfloat16
+I32 = mybir.dt.int32
+U32 = mybir.dt.uint32
+U16 = mybir.dt.uint16
+U8 = mybir.dt.uint8
+FP8X4 = mybir.dt.float8_e4m3fn_x4
+MAX = mybir.AluOpType.max
+MIN = mybir.AluOpType.min
+
+P = 128
+PACK = 4
+LIST = 16
+W_PIECES = (128, 128, 128, 64, 64)
+HALF_S = S // 2
+HALF_V = V // 2
+
+
+def tile_picked_median_none_lo_kernel(
+    tc, xT, w1, offs, pos1, pos2, pos3, out_0, out_1, out_2
+):
+    nc = tc.nc
+    with ExitStack() as ctx:
+        sb = ctx.enter_context(tc.tile_pool(name="sb", bufs=1))
+        ps = ctx.enter_context(tc.psum_pool(name="ps", bufs=1))
+
+        x_rows = xT.rearrange("(p j) c -> p j c", j=PACK)
+        w_rows = w1.rearrange("(p j) c -> p j c", j=PACK)
+        out_rows = out_0.rearrange("(p t) v -> p t v", t=PACK)
+        out_words = out_1[0].rearrange("p c r -> p (c r)").bitcast(I32)
+        out_scales = out_2[0].bitcast(I32)
+
+        x_raw = [sb.tile([P, T], F32, name="x_raw%d" % j) for j in range(PACK)]
+        picked = sb.tile([P, S // LIST], U16, name="picked")
+        nc.sync.dma_start(out=x_raw[0][:], in_=x_rows[:, 0, :])
+        nc.sync.dma_start(picked[:], offs)
+        for j in range(1, PACK):
+            nc.sync.dma_start(out=x_raw[j][:], in_=x_rows[:, j, :])
+        w_raw = []
+        first = 0
+        for i, width in enumerate(W_PIECES):
+            piece = sb.tile([P, PACK, width], F32, name="w_raw%d" % i)
+            nc.sync.dma_start(out=piece[:], in_=w_rows[:, :, first : first + width])
+            w_raw.append((piece, first, width))
+            first = first + width
+        places = []
+        for i, pos in enumerate((pos1, pos2, pos3)):
+            place = sb.tile([P, V // LIST], U16, name="place%d" % i)
+            nc.sync.dma_start(place[:], pos)
+            places.append(place)
+
+        pairs = [sb.tile([P, 2, S], F32, name="x_pair%d" % u) for u in range(2)]
+        x_bf = sb.tile([P, S, PACK], BF16, name="x_bf", align_bytes=64)
+        x_codes = sb.tile([P, S], U32, name="x_codes", align_bytes=64)
+        x_scales = sb.tile([P, S], U8, name="x_scales", align_bytes=64)
+
+        def weave(engine_copy, dst, src):
+            engine_copy(
+                out=dst.rearrange("p (c i) e -> p c e i", i=4),
+                in_=src.rearrange("p e (c i) -> p c e i", i=4),
+            )
+
+        for j in range(PACK - 1):
+            nc.vector.tensor_copy(pairs[j // 2][:, j % 2, :], x_raw[j][:].indirect(picked[:]))
+        weave(nc.scalar.copy, x_bf[:, :, 0:2], pairs[0][:])
+        halves = [slice(h * HALF_S, (h + 1) * HALF_S) for h in range(2)]
+        for h in range(2):
+            cols = slice(h * HALF_S // LIST, (h + 1) * HALF_S // LIST)
+            nc.vector.tensor_copy(pairs[1][:, 1, halves[h]], x_raw[3][:].indirect(picked[:, cols]))
+        for h in range(2):
+            weave(nc.vector.tensor_copy, x_bf[:, halves[h], 2:4], pairs[1][:, :, halves[h]])
+        for h in range(2):
+            nc.vector.quantize_mx(
+                out=x_codes[:, halves[h]].bitcast(FP8X4),
+                scales=x_scales[:, halves[h]],
+                in_=x_bf[:, halves[h], :].rearrange("p s j -> p (s j)"),
+            )
+
+        w_bf = sb.tile([P, PACK, P, PACK], BF16, name="w_bf", align_bytes=64)
+        w_codes = sb.tile([P, PACK, P], U32, name="w_codes", align_bytes=64)
+        w_scales = sb.tile([P, PACK, P], U8, name="w_scales", align_bytes=64)
+        for piece, first, width in w_raw:
+            ms = slice(first // PACK, (first + width) // PACK)
+            nc.scalar.copy(
+                out=w_bf[:, :, ms, :].rearrange("p t m j -> p m j t"),
+                in_=piece[:].rearrange("p j (m t) -> p m j t", t=PACK),
+            )
+        for t in range(PACK):
+            nc.vector.quantize_mx(
+                out=w_codes[:, t, :].bitcast(FP8X4),
+                scales=w_scales[:, t, :],
+                in_=w_bf[:, t, :, :].rearrange("p m j -> p (m j)"),
+            )
+
+        y = [sb.tile([P, S], F32, name="y%d" % t) for t in range(PACK)]
+
+        def product(name, t, cols, engine_copy):
+            acc = ps.tile([P, cols.stop - cols.start], F32, name=name)
+            nc.tensor.matmul_mx(
+                out=acc[:],
+                lhsT=w_codes[:, t, :].bitcast(FP8X4),
+                lhsT_scale=w_scales[:, t, :],
+                rhs=x_codes[:, cols].bitcast(FP8X4),
+                rhs_scale=x_scales[:, cols],
+                start=True,
+                stop=True,
+            )
+            engine_copy(out=y[t][:, cols], in_=acc[:])
+
+        product("acc0a", 0, halves[0], nc.scalar.copy)
+        product("acc0b", 0, halves[1], nc.vector.tensor_copy)
+        for t in range(1, PACK):
+            product("acc%d" % t, t, slice(0, S), nc.scalar.copy)
+
+        med = [sb.tile([P, 2, V], F32, name="med%d" % u) for u in range(2)]
+        o_bf = sb.tile([P, V, PACK], BF16, name="o_bf", align_bytes=64)
+        o_codes = sb.tile([P, V], U32, name="o_codes", align_bytes=64)
+        o_scales = sb.tile([P, V], U8, name="o_scales", align_bytes=64)
+
+        jobs = [(t, slice(0, V)) for t in range(PACK - 1)]
+        jobs = jobs + [(PACK - 1, slice(0, HALF_V)), (PACK - 1, slice(HALF_V, V))]
+
+        def fetch(n, i):
+            t, vs = jobs[n]
+            got = sb.tile([P, vs.stop - vs.start], F32, name="got%d_%d" % (n, i))
+            cols = slice(vs.start // LIST, vs.stop // LIST)
+            nc.vector.tensor_copy(got[:], y[t][:].indirect(places[i][:, cols]))
+            return got
+
+        def close(n, low, capped):
+            t, vs = jobs[n]
+            nc.vector.tensor_tensor(med[t // 2][:, t % 2, vs], low[:], capped[:], MAX)
+            nc.sync.dma_start(out=out_rows[:, t, vs], in_=med[t // 2][:, t % 2, vs])
+            if t == 1:
+                weave(nc.scalar.copy, o_bf[:, :, 0:2], med[0][:])
+            if t == PACK - 1:
+                last = vs.stop == V
+                weave(nc.vector.tensor_copy if last else nc.scalar.copy, o_bf[:, vs, 2:4], med[1][:, :, vs])
+                nc.vector.quantize_mx(
+                    out=o_codes[:, vs].bitcast(FP8X4),
+                    scales=o_scales[:, vs],
+                    in_=o_bf[:, vs, :].rearrange("p v t -> p (v t)"),
+                )
+                nc.scalar.dma_start(out=out_words[:, vs], in_=o_codes[:, vs].bitcast(I32))
+
+        pending = None
+        for n, (t, vs) in enumerate(jobs):
+            width = vs.stop - vs.start
+            a = fetch(n, 0)
+            if pending is not None:
+                close(*pending)
+            b = fetch(n, 1)
+            c = fetch(n, 2)
+            high = sb.tile([P, width], F32, name="high%d" % n)
+            low = sb.tile([P, width], F32, name="low%d" % n)
+            capped = sb.tile([P, width], F32, name="capped%d" % n)
+            nc.vector.tensor_tensor(high[:], a[:], b[:], MAX)
+            nc.vector.tensor_tensor(low[:], a[:], b[:], MIN)
+            nc.vector.tensor_tensor(capped[:], high[:], c[:], MIN)
+            pending = (n, low, capped)
+        close(*pending)
+
+        scale_rows = o_scales[:].bitcast(I32)
+        for q in range(4):
+            queue = nc.sync if q % 2 == 0 else nc.scalar
+            queue.dma_start(out=out_scales[4 * q : 4 * q + 4, :], in_=scale_rows[32 * q : 32 * q + 4, :])

@@ -18,7 +18,7 @@ MIN = mybir.AluOpType.min
 P = 128
 PACK = 4
 LIST = 16
-W_PIECES = (128, 128, 128, 64, 64)
+W_PIECES = (128, 128, 128, 128)
 HALF_S = S // 2
 HALF_V = V // 2
 
@@ -56,7 +56,7 @@ def tile_picked_median_none_lo_kernel(
             nc.sync.dma_start(place[:], pos)
             places.append(place)
 
-        pairs = [sb.tile([P, 2, S], F32, name="x_pair%d" % u) for u in range(2)]
+        pairs = [sb.tile([P, 2, S], F32, name="x_pair%d" % u, tag="stage%d" % u, align_bytes=64) for u in range(2)]
         x_bf = sb.tile([P, S, PACK], BF16, name="x_bf", align_bytes=64)
         x_codes = sb.tile([P, S], U32, name="x_codes", align_bytes=64)
         x_scales = sb.tile([P, S], U8, name="x_scales", align_bytes=64)
@@ -67,36 +67,42 @@ def tile_picked_median_none_lo_kernel(
                 in_=src.rearrange("p e (c i) -> p c e i", i=4),
             )
 
-        for j in range(PACK - 1):
-            nc.vector.tensor_copy(pairs[j // 2][:, j % 2, :], x_raw[j][:].indirect(picked[:]))
-        weave(nc.scalar.copy, x_bf[:, :, 0:2], pairs[0][:])
         halves = [slice(h * HALF_S, (h + 1) * HALF_S) for h in range(2)]
-        for h in range(2):
-            cols = slice(h * HALF_S // LIST, (h + 1) * HALF_S // LIST)
-            nc.vector.tensor_copy(pairs[1][:, 1, halves[h]], x_raw[3][:].indirect(picked[:, cols]))
-        for h in range(2):
-            weave(nc.vector.tensor_copy, x_bf[:, halves[h], 2:4], pairs[1][:, :, halves[h]])
-        for h in range(2):
+        for u, engine_copy in enumerate((nc.scalar.copy, nc.vector.tensor_copy)):
+            nc.vector.tensor_copy(pairs[u][:, 0, :], x_raw[2 * u][:].indirect(picked[:]))
+            for half in halves:
+                cols = slice(half.start // LIST, half.stop // LIST)
+                nc.vector.tensor_copy(pairs[u][:, 1, half], x_raw[2 * u + 1][:].indirect(picked[:, cols]))
+            for half in halves:
+                weave(engine_copy, x_bf[:, half, 2 * u : 2 * u + 2], pairs[u][:, :, half])
+
+        def quantize_x(cols):
             nc.vector.quantize_mx(
-                out=x_codes[:, halves[h]].bitcast(FP8X4),
-                scales=x_scales[:, halves[h]],
-                in_=x_bf[:, halves[h], :].rearrange("p s j -> p (s j)"),
+                out=x_codes[:, cols].bitcast(FP8X4),
+                scales=x_scales[:, cols],
+                in_=x_bf[:, cols, :].rearrange("p s j -> p (s j)"),
             )
 
-        w_bf = sb.tile([P, PACK, P, PACK], BF16, name="w_bf", align_bytes=64)
+        w_bf = sb.tile([P, PACK, P, PACK], BF16, name="w_bf", tag="stage0", align_bytes=64)
         w_codes = sb.tile([P, PACK, P], U32, name="w_codes", align_bytes=64)
         w_scales = sb.tile([P, PACK, P], U8, name="w_scales", align_bytes=64)
-        for piece, first, width in w_raw:
-            ms = slice(first // PACK, (first + width) // PACK)
-            nc.scalar.copy(
+
+        def deal(engine_copy, piece, first, cols):
+            ms = slice((first + cols.start) // PACK, (first + cols.stop) // PACK)
+            engine_copy(
                 out=w_bf[:, :, ms, :].rearrange("p t m j -> p m j t"),
-                in_=piece[:].rearrange("p j (m t) -> p m j t", t=PACK),
+                in_=piece[:, :, cols].rearrange("p j (m t) -> p m j t", t=PACK),
             )
-        for t in range(PACK):
+
+        for half in halves:
+            quantize_x(half)
+        for piece, first, width in w_raw:
+            deal(nc.scalar.copy, piece, first, slice(0, width))
+        for ts in (slice(0, 1), slice(1, 2), slice(2, 4)):
             nc.vector.quantize_mx(
-                out=w_codes[:, t, :].bitcast(FP8X4),
-                scales=w_scales[:, t, :],
-                in_=w_bf[:, t, :, :].rearrange("p m j -> p (m j)"),
+                out=w_codes[:, ts, :].rearrange("p t m -> p (t m)").bitcast(FP8X4),
+                scales=w_scales[:, ts, :].rearrange("p t m -> p (t m)"),
+                in_=w_bf[:, ts, :, :].rearrange("p t m j -> p (t m j)"),
             )
 
         y = [sb.tile([P, S], F32, name="y%d" % t) for t in range(PACK)]
@@ -124,48 +130,65 @@ def tile_picked_median_none_lo_kernel(
         o_codes = sb.tile([P, V], U32, name="o_codes", align_bytes=64)
         o_scales = sb.tile([P, V], U8, name="o_scales", align_bytes=64)
 
-        jobs = [(t, slice(0, V)) for t in range(PACK - 1)]
-        jobs = jobs + [(PACK - 1, slice(0, HALF_V)), (PACK - 1, slice(HALF_V, V))]
+        groups = [
+            [(0, slice(0, V)), (1, slice(0, V))],
+            [(2, slice(0, V))],
+            [(3, slice(0, HALF_V))],
+            [(3, slice(HALF_V, V))],
+        ]
 
-        def fetch(n, i):
-            t, vs = jobs[n]
-            got = sb.tile([P, vs.stop - vs.start], F32, name="got%d_%d" % (n, i))
+        def span(n):
+            t0, vs0 = groups[n][0]
+            t1, vs1 = groups[n][-1]
+            return slice((t0 % 2) * V + vs0.start, (t1 % 2) * V + vs1.stop)
+
+        def fetch(n, got, i, k):
+            t, vs = groups[n][k]
+            first = (t % 2) * V - span(n).start
             cols = slice(vs.start // LIST, vs.stop // LIST)
-            nc.vector.tensor_copy(got[:], y[t][:].indirect(places[i][:, cols]))
-            return got
+            nc.vector.tensor_copy(got[i][:, first + vs.start : first + vs.stop], y[t][:].indirect(places[i][:, cols]))
 
         def close(n, low, capped):
-            t, vs = jobs[n]
-            nc.vector.tensor_tensor(med[t // 2][:, t % 2, vs], low[:], capped[:], MAX)
-            nc.sync.dma_start(out=out_rows[:, t, vs], in_=med[t // 2][:, t % 2, vs])
-            if t == 1:
-                weave(nc.scalar.copy, o_bf[:, :, 0:2], med[0][:])
-            if t == PACK - 1:
-                last = vs.stop == V
-                weave(nc.vector.tensor_copy if last else nc.scalar.copy, o_bf[:, vs, 2:4], med[1][:, :, vs])
-                nc.vector.quantize_mx(
-                    out=o_codes[:, vs].bitcast(FP8X4),
-                    scales=o_scales[:, vs],
-                    in_=o_bf[:, vs, :].rearrange("p v t -> p (v t)"),
-                )
-                nc.scalar.dma_start(out=out_words[:, vs], in_=o_codes[:, vs].bitcast(I32))
+            pair = med[groups[n][0][0] // 2]
+            nc.vector.tensor_tensor(pair[:].rearrange("p t v -> p (t v)")[:, span(n)], low[:], capped[:], MAX)
+            if n == 0:
+                nc.sync.dma_start(out=out_rows[:, 0:2, :], in_=pair[:])
+                weave(nc.scalar.copy, o_bf[:, :, 0:2], pair[:])
+            else:
+                for t, vs in groups[n]:
+                    nc.sync.dma_start(out=out_rows[:, t, vs], in_=pair[:, t % 2, vs])
+                t, vs = groups[n][-1]
+                if t == PACK - 1:
+                    weave(nc.vector.tensor_copy if vs.stop == V else nc.scalar.copy, o_bf[:, vs, 2:4], pair[:, :, vs])
+
+        def hand_on(vs):
+            nc.vector.quantize_mx(
+                out=o_codes[:, vs].bitcast(FP8X4),
+                scales=o_scales[:, vs],
+                in_=o_bf[:, vs, :].rearrange("p v t -> p (v t)"),
+            )
+            nc.scalar.dma_start(out=out_words[:, vs], in_=o_codes[:, vs].bitcast(I32))
 
         pending = None
-        for n, (t, vs) in enumerate(jobs):
-            width = vs.stop - vs.start
-            a = fetch(n, 0)
+        for n, group in enumerate(groups):
+            width = span(n).stop - span(n).start
+            got = [sb.tile([P, width], F32, name="got%d_%d" % (n, i)) for i in range(3)]
+            steps = [(i, k) for k in range(len(group)) for i in range(3)]
+            fetch(n, got, *steps[0])
             if pending is not None:
                 close(*pending)
-            b = fetch(n, 1)
-            c = fetch(n, 2)
+            for i, k in steps[1:]:
+                fetch(n, got, i, k)
             high = sb.tile([P, width], F32, name="high%d" % n)
             low = sb.tile([P, width], F32, name="low%d" % n)
             capped = sb.tile([P, width], F32, name="capped%d" % n)
-            nc.vector.tensor_tensor(high[:], a[:], b[:], MAX)
-            nc.vector.tensor_tensor(low[:], a[:], b[:], MIN)
-            nc.vector.tensor_tensor(capped[:], high[:], c[:], MIN)
+            nc.vector.tensor_tensor(high[:], got[0][:], got[1][:], MAX)
+            nc.vector.tensor_tensor(low[:], got[0][:], got[1][:], MIN)
+            nc.vector.tensor_tensor(capped[:], high[:], got[2][:], MIN)
             pending = (n, low, capped)
+        hand_on(slice(0, HALF_V))
         close(*pending)
+        hand_on(slice(HALF_V, V))
 
         scale_rows = o_scales[:].bitcast(I32)
         for q in range(4):

@@ -18,7 +18,7 @@ MIN = mybir.AluOpType.min
 P = 128
 PACK = 4
 LIST = 16
-W_PIECES = (128, 128, 128, 128)
+W_PIECES = (256, 256)
 HALF_S = S // 2
 HALF_V = V // 2
 
@@ -87,17 +87,18 @@ def tile_picked_median_none_lo_kernel(
         w_codes = sb.tile([P, PACK, P], U32, name="w_codes", align_bytes=64)
         w_scales = sb.tile([P, PACK, P], U8, name="w_scales", align_bytes=64)
 
-        def deal(engine_copy, piece, first, cols):
-            ms = slice((first + cols.start) // PACK, (first + cols.stop) // PACK)
+        def deal(engine_copy, piece, first, width, ts):
+            ms = slice(first // PACK, (first + width) // PACK)
             engine_copy(
-                out=w_bf[:, :, ms, :].rearrange("p t m j -> p m j t"),
-                in_=piece[:, :, cols].rearrange("p j (m t) -> p m j t", t=PACK),
+                out=w_bf[:, ts, ms, :].rearrange("p t m j -> p m j t"),
+                in_=piece[:].rearrange("p j (m t) -> p m j t", t=PACK)[:, :, :, ts],
             )
 
         for half in halves:
             quantize_x(half)
-        for piece, first, width in w_raw:
-            deal(nc.scalar.copy, piece, first, slice(0, width))
+        deal(nc.scalar.copy, *w_raw[0], slice(0, PACK))
+        deal(nc.scalar.copy, *w_raw[1], slice(0, 2))
+        deal(nc.scalar.copy, *w_raw[1], slice(2, PACK))
         for ts in (slice(0, 1), slice(1, 2), slice(2, 4)):
             nc.vector.quantize_mx(
                 out=w_codes[:, ts, :].rearrange("p t m -> p (t m)").bitcast(FP8X4),
@@ -120,8 +121,8 @@ def tile_picked_median_none_lo_kernel(
             )
             engine_copy(out=y[t][:, cols], in_=acc[:])
 
-        product("acc0a", 0, halves[0], nc.scalar.copy)
-        product("acc0b", 0, halves[1], nc.vector.tensor_copy)
+        product("acc0a", 0, halves[0], nc.vector.tensor_copy)
+        product("acc0b", 0, halves[1], nc.scalar.copy)
         for t in range(1, PACK):
             product("acc%d" % t, t, slice(0, S), nc.scalar.copy)
 

@@ -56,10 +56,12 @@ def tile_picked_median_none_lo_kernel(
             nc.sync.dma_start(place[:], pos)
             places.append(place)
 
-        pairs = [sb.tile([P, 2, S], F32, name="x_pair%d" % u, tag="stage%d" % u, align_bytes=64) for u in range(2)]
-        x_bf = sb.tile([P, S, PACK], BF16, name="x_bf", align_bytes=64)
-        x_codes = sb.tile([P, S], U32, name="x_codes", align_bytes=64)
-        x_scales = sb.tile([P, S], U8, name="x_scales", align_bytes=64)
+        pairs = [sb.tile([P, 2, S], F32, name="x_pair%d" % u) for u in range(2)]
+        rounded = sb.tile([P, (S + N) * PACK], BF16, name="rounded", align_bytes=64)
+        codes = sb.tile([P, S + N], U32, name="codes", align_bytes=64)
+        scales = sb.tile([P, S + N], U8, name="scales", align_bytes=64)
+        x_bf = rounded[:, 0 : S * PACK].rearrange("p (s j) -> p s j", j=PACK)
+        w_bf = rounded[:, S * PACK :].rearrange("p (t m j) -> p t m j", t=PACK, j=PACK)
 
         def weave(engine_copy, dst, src):
             engine_copy(
@@ -76,16 +78,12 @@ def tile_picked_median_none_lo_kernel(
             for half in halves:
                 weave(engine_copy, x_bf[:, half, 2 * u : 2 * u + 2], pairs[u][:, :, half])
 
-        def quantize_x(cols):
+        def quantize(first, stop):
             nc.vector.quantize_mx(
-                out=x_codes[:, cols].bitcast(FP8X4),
-                scales=x_scales[:, cols],
-                in_=x_bf[:, cols, :].rearrange("p s j -> p (s j)"),
+                out=codes[:, first:stop].bitcast(FP8X4),
+                scales=scales[:, first:stop],
+                in_=rounded[:, first * PACK : stop * PACK],
             )
-
-        w_bf = sb.tile([P, PACK, P, PACK], BF16, name="w_bf", tag="stage0", align_bytes=64)
-        w_codes = sb.tile([P, PACK, P], U32, name="w_codes", align_bytes=64)
-        w_scales = sb.tile([P, PACK, P], U8, name="w_scales", align_bytes=64)
 
         def deal(engine_copy, piece, first, width, ts):
             ms = slice(first // PACK, (first + width) // PACK)
@@ -94,17 +92,14 @@ def tile_picked_median_none_lo_kernel(
                 in_=piece[:].rearrange("p j (m t) -> p m j t", t=PACK)[:, :, :, ts],
             )
 
-        for half in halves:
-            quantize_x(half)
+        quantize(0, HALF_S)
+        quantize(HALF_S, S - P)
         deal(nc.scalar.copy, *w_raw[0], slice(0, PACK))
         deal(nc.scalar.copy, *w_raw[1], slice(0, 2))
         deal(nc.scalar.copy, *w_raw[1], slice(2, PACK))
-        for ts in (slice(0, 1), slice(1, 2), slice(2, 4)):
-            nc.vector.quantize_mx(
-                out=w_codes[:, ts, :].rearrange("p t m -> p (t m)").bitcast(FP8X4),
-                scales=w_scales[:, ts, :].rearrange("p t m -> p (t m)"),
-                in_=w_bf[:, ts, :, :].rearrange("p t m j -> p (t m j)"),
-            )
+        quantize(S + P, S + 2 * P)
+        quantize(S - P, S + P)
+        quantize(S + 2 * P, S + N)
 
         y = [sb.tile([P, S], F32, name="y%d" % t) for t in range(PACK)]
 
@@ -112,18 +107,18 @@ def tile_picked_median_none_lo_kernel(
             acc = ps.tile([P, cols.stop - cols.start], F32, name=name)
             nc.tensor.matmul_mx(
                 out=acc[:],
-                lhsT=w_codes[:, t, :].bitcast(FP8X4),
-                lhsT_scale=w_scales[:, t, :],
-                rhs=x_codes[:, cols].bitcast(FP8X4),
-                rhs_scale=x_scales[:, cols],
+                lhsT=codes[:, S + t * P : S + (t + 1) * P].bitcast(FP8X4),
+                lhsT_scale=scales[:, S + t * P : S + (t + 1) * P],
+                rhs=codes[:, cols].bitcast(FP8X4),
+                rhs_scale=scales[:, cols],
                 start=True,
                 stop=True,
             )
             engine_copy(out=y[t][:, cols], in_=acc[:])
 
-        product("acc0a", 0, halves[0], nc.vector.tensor_copy)
-        product("acc0b", 0, halves[1], nc.scalar.copy)
-        for t in range(1, PACK):
+        for first in range(0, S, P):
+            product("acc1_%d" % first, 1, slice(first, first + P), nc.scalar.copy)
+        for t in (0, 2, 3):
             product("acc%d" % t, t, slice(0, S), nc.scalar.copy)
 
         med = [sb.tile([P, 2, V], F32, name="med%d" % u) for u in range(2)]
@@ -174,7 +169,7 @@ def tile_picked_median_none_lo_kernel(
         for n, group in enumerate(groups):
             width = span(n).stop - span(n).start
             got = [sb.tile([P, width], F32, name="got%d_%d" % (n, i)) for i in range(3)]
-            steps = [(i, k) for k in range(len(group)) for i in range(3)]
+            steps = [(i, k) for k in reversed(range(len(group))) for i in range(3)]
             fetch(n, got, *steps[0])
             if pending is not None:
                 close(*pending)

@@ -116,8 +116,9 @@ def tile_picked_median_none_lo_kernel(
             )
             engine_copy(out=y[t][:, cols], in_=acc[:])
 
-        for first in range(0, S, P):
-            product("acc1_%d" % first, 1, slice(first, first + P), nc.scalar.copy)
+        product("acc1a", 1, halves[0], nc.vector.tensor_copy)
+        product("acc1b", 1, slice(HALF_S, S - P), nc.scalar.copy)
+        product("acc1c", 1, slice(S - P, S), nc.scalar.copy)
         for t in (0, 2, 3):
             product("acc%d" % t, t, slice(0, S), nc.scalar.copy)
 

@@ -19,6 +19,7 @@ P = 128
 PACK = 4
 LIST = 16
 W_PIECES = (256, 256)
+SCALAR_SHARE = 96
 HALF_S = S // 2
 HALF_V = V // 2
 
@@ -48,7 +49,7 @@ def tile_picked_median_none_lo_kernel(
         for i, width in enumerate(W_PIECES):
             piece = sb.tile([P, PACK, width], F32, name="w_raw%d" % i)
             nc.sync.dma_start(out=piece[:], in_=w_rows[:, :, first : first + width])
-            w_raw.append((piece, first, width))
+            w_raw.append((piece, first))
             first = first + width
         places = []
         for i, pos in enumerate((pos1, pos2, pos3)):
@@ -85,18 +86,19 @@ def tile_picked_median_none_lo_kernel(
                 in_=rounded[:, first * PACK : stop * PACK],
             )
 
-        def deal(engine_copy, piece, first, width, ts):
-            ms = slice(first // PACK, (first + width) // PACK)
+        def deal(engine_copy, piece, first, cols, ts):
+            ms = slice((first + cols.start) // PACK, (first + cols.stop) // PACK)
             engine_copy(
                 out=w_bf[:, ts, ms, :].rearrange("p t m j -> p m j t"),
-                in_=piece[:].rearrange("p j (m t) -> p m j t", t=PACK)[:, :, :, ts],
+                in_=piece[:, :, cols].rearrange("p j (m t) -> p m j t", t=PACK)[:, :, :, ts],
             )
 
         quantize(0, HALF_S)
         quantize(HALF_S, S - P)
-        deal(nc.scalar.copy, *w_raw[0], slice(0, PACK))
-        deal(nc.scalar.copy, *w_raw[1], slice(0, 2))
-        deal(nc.scalar.copy, *w_raw[1], slice(2, PACK))
+        deal(nc.scalar.copy, *w_raw[0], slice(0, W_PIECES[0]), slice(0, PACK))
+        deal(nc.scalar.copy, *w_raw[1], slice(0, SCALAR_SHARE), slice(0, 2))
+        deal(nc.vector.tensor_copy, *w_raw[1], slice(SCALAR_SHARE, W_PIECES[1]), slice(0, 2))
+        deal(nc.scalar.copy, *w_raw[1], slice(0, W_PIECES[1]), slice(2, PACK))
         quantize(S + P, S + 2 * P)
         quantize(S - P, S + P)
         quantize(S + 2 * P, S + N)

@@ -1,6 +1,7 @@
 from contextlib import ExitStack
 
 import concourse.mybir as mybir
+from concourse.masks import make_identity
 
 K, T, S, V, N = 512, 1024, 512, 256, 512
 FLOPS = 2 * K * N * S
@@ -18,8 +19,9 @@ MIN = mybir.AluOpType.min
 P = 128
 PACK = 4
 LIST = 16
-W_PIECES = (256, 256)
-SCALAR_SHARE = 96
+HALF_N = N // 2
+HALF_P = P // 2
+EARLY = 320
 HALF_S = S // 2
 HALF_V = V // 2
 
@@ -44,13 +46,9 @@ def tile_picked_median_none_lo_kernel(
         nc.sync.dma_start(picked[:], offs)
         for j in range(1, PACK):
             nc.sync.dma_start(out=x_raw[j][:], in_=x_rows[:, j, :])
-        w_raw = []
-        first = 0
-        for i, width in enumerate(W_PIECES):
-            piece = sb.tile([P, PACK, width], F32, name="w_raw%d" % i)
-            nc.sync.dma_start(out=piece[:], in_=w_rows[:, :, first : first + width])
-            w_raw.append((piece, first))
-            first = first + width
+        w_raw = [sb.tile([P, PACK, HALF_N], F32, name="w_raw%d" % h) for h in range(2)]
+        for h in range(2):
+            nc.sync.dma_start(out=w_raw[h][:], in_=w_rows[:, :, h * HALF_N : (h + 1) * HALF_N])
         places = []
         for i, pos in enumerate((pos1, pos2, pos3)):
             place = sb.tile([P, V // LIST], U16, name="place%d" % i)
@@ -62,7 +60,9 @@ def tile_picked_median_none_lo_kernel(
         codes = sb.tile([P, S + N], U32, name="codes", align_bytes=64)
         scales = sb.tile([P, S + N], U8, name="scales", align_bytes=64)
         x_bf = rounded[:, 0 : S * PACK].rearrange("p (s j) -> p s j", j=PACK)
-        w_bf = rounded[:, S * PACK :].rearrange("p (t m j) -> p t m j", t=PACK, j=PACK)
+        first_col = {2: S, 3: S + P, 0: S + 2 * P, 1: S + 3 * P}
+        w_straight = rounded[:, S * PACK : (S + 2 * P) * PACK].rearrange("p (t m j) -> p t m j", t=2, j=PACK)
+        w_mixed = rounded[:, (S + 2 * P) * PACK :].rearrange("p (h t m j) -> p h t m j", h=2, t=2, j=PACK)
 
         def weave(engine_copy, dst, src):
             engine_copy(
@@ -70,14 +70,14 @@ def tile_picked_median_none_lo_kernel(
                 in_=src.rearrange("p e (c i) -> p c e i", i=4),
             )
 
-        halves = [slice(h * HALF_S, (h + 1) * HALF_S) for h in range(2)]
+        parts = [slice(0, EARLY), slice(EARLY, S)]
         for u, engine_copy in enumerate((nc.scalar.copy, nc.vector.tensor_copy)):
             nc.vector.tensor_copy(pairs[u][:, 0, :], x_raw[2 * u][:].indirect(picked[:]))
-            for half in halves:
-                cols = slice(half.start // LIST, half.stop // LIST)
-                nc.vector.tensor_copy(pairs[u][:, 1, half], x_raw[2 * u + 1][:].indirect(picked[:, cols]))
-            for half in halves:
-                weave(engine_copy, x_bf[:, half, 2 * u : 2 * u + 2], pairs[u][:, :, half])
+            for part in parts:
+                cols = slice(part.start // LIST, part.stop // LIST)
+                nc.vector.tensor_copy(pairs[u][:, 1, part], x_raw[2 * u + 1][:].indirect(picked[:, cols]))
+            for part in parts:
+                weave(engine_copy, x_bf[:, part, 2 * u : 2 * u + 2], pairs[u][:, :, part])
 
         def quantize(first, stop):
             nc.vector.quantize_mx(
@@ -86,31 +86,21 @@ def tile_picked_median_none_lo_kernel(
                 in_=rounded[:, first * PACK : stop * PACK],
             )
 
-        def deal(engine_copy, piece, first, cols, ts):
-            ms = slice((first + cols.start) // PACK, (first + cols.stop) // PACK)
-            engine_copy(
-                out=w_bf[:, ts, ms, :].rearrange("p t m j -> p m j t"),
-                in_=piece[:, :, cols].rearrange("p j (m t) -> p m j t", t=PACK)[:, :, :, ts],
+        def deal(dst, h, ts):
+            nc.scalar.copy(
+                out=dst.rearrange("p t m j -> p m j t"),
+                in_=w_raw[h][:].rearrange("p j (m t) -> p m j t", t=PACK)[:, :, :, ts],
             )
-
-        quantize(0, HALF_S)
-        quantize(HALF_S, S - P)
-        deal(nc.scalar.copy, *w_raw[0], slice(0, W_PIECES[0]), slice(0, PACK))
-        deal(nc.scalar.copy, *w_raw[1], slice(0, SCALAR_SHARE), slice(0, 2))
-        deal(nc.vector.tensor_copy, *w_raw[1], slice(SCALAR_SHARE, W_PIECES[1]), slice(0, 2))
-        deal(nc.scalar.copy, *w_raw[1], slice(0, W_PIECES[1]), slice(2, PACK))
-        quantize(S + P, S + 2 * P)
-        quantize(S - P, S + P)
-        quantize(S + 2 * P, S + N)
 
         y = [sb.tile([P, S], F32, name="y%d" % t) for t in range(PACK)]
 
         def product(name, t, cols, engine_copy):
-            acc = ps.tile([P, cols.stop - cols.start], F32, name=name)
+            acc = ps.tile([P, cols.stop - cols.start], F32, name=name, tag=name)
+            w_cols = slice(first_col[t], first_col[t] + P)
             nc.tensor.matmul_mx(
                 out=acc[:],
-                lhsT=codes[:, S + t * P : S + (t + 1) * P].bitcast(FP8X4),
-                lhsT_scale=scales[:, S + t * P : S + (t + 1) * P],
+                lhsT=codes[:, w_cols].bitcast(FP8X4),
+                lhsT_scale=scales[:, w_cols],
                 rhs=codes[:, cols].bitcast(FP8X4),
                 rhs_scale=scales[:, cols],
                 start=True,
@@ -118,13 +108,30 @@ def tile_picked_median_none_lo_kernel(
             )
             engine_copy(out=y[t][:, cols], in_=acc[:])
 
-        product("acc1a", 1, halves[0], nc.vector.tensor_copy)
-        product("acc1b", 1, slice(HALF_S, S - P), nc.scalar.copy)
-        product("acc1c", 1, slice(S - P, S), nc.scalar.copy)
-        for t in (0, 2, 3):
+        quantize(0, HALF_P)
+        quantize(HALF_P, EARLY)
+        deal(w_mixed[:, 0], 0, slice(0, 2))
+        quantize(first_col[0], first_col[0] + P)
+        deal(w_straight[:, :, 0:HALF_P, :], 0, slice(2, PACK))
+        quantize(EARLY, S + HALF_P)
+        product("acc0a", 0, slice(0, HALF_S), nc.vector.tensor_copy)
+        product("acc0b", 0, slice(HALF_S, S - P), nc.scalar.copy)
+        product("acc0c", 0, slice(S - P, S), nc.scalar.copy)
+        quantize(first_col[3], first_col[3] + HALF_P)
+        deal(w_mixed[:, 1], 1, slice(0, 2))
+        quantize(first_col[1], first_col[1] + P)
+        product("acc1", 1, slice(0, S), nc.scalar.copy)
+        deal(w_straight[:, :, HALF_P:P, :], 1, slice(2, PACK))
+        for t in (2, 3):
+            quantize(first_col[t] + HALF_P, first_col[t] + P)
             product("acc%d" % t, t, slice(0, S), nc.scalar.copy)
 
-        med = [sb.tile([P, 2, V], F32, name="med%d" % u) for u in range(2)]
+        identity = sb.tile([P, P], F32, name="identity")
+        make_identity(nc, identity[:])
+        mixed = sb.tile([P, 2, V], F32, name="mixed")
+        straight = sb.tile([P, 2, V], F32, name="straight")
+        out_mixed = out_0.rearrange("(h m t) v -> t m h v", h=2, t=PACK)
+        sides = [slice(0, HALF_P), slice(HALF_P, P)]
         o_bf = sb.tile([P, V, PACK], BF16, name="o_bf", align_bytes=64)
         o_codes = sb.tile([P, V], U32, name="o_codes", align_bytes=64)
         o_scales = sb.tile([P, V], U8, name="o_scales", align_bytes=64)
@@ -147,18 +154,35 @@ def tile_picked_median_none_lo_kernel(
             cols = slice(vs.start // LIST, vs.stop // LIST)
             nc.vector.tensor_copy(got[i][:, first + vs.start : first + vs.stop], y[t][:].indirect(places[i][:, cols]))
 
+        def regroup(b):
+            vs = slice(b * HALF_V, (b + 1) * HALF_V)
+            across = ps.tile([P, 2, P], F32, name="across%d" % b, tag="acc0%s" % "ab"[b])
+            for h in range(2):
+                nc.tensor.transpose(across[:, h, :], mixed[:, h, vs], identity[:])
+            turned = sb.tile([P, 2, P], F32, name="turned%d" % b)
+            nc.scalar.copy(
+                out=turned[:].rearrange("p t (h m) -> p t h m", h=2),
+                in_=across[:].rearrange("p h (t m) -> p t h m", t=2),
+            )
+            back = ps.tile([P, 2, HALF_V], F32, name="back%d" % b)
+            for t in range(2):
+                nc.tensor.transpose(back[:, t, :], turned[:, t, :], identity[:])
+            weave(nc.scalar.copy, o_bf[:, vs, 0:2], back[:])
+
         def close(n, low, capped):
-            pair = med[groups[n][0][0] // 2]
-            nc.vector.tensor_tensor(pair[:].rearrange("p t v -> p (t v)")[:, span(n)], low[:], capped[:], MAX)
             if n == 0:
-                nc.sync.dma_start(out=out_rows[:, 0:2, :], in_=pair[:])
-                weave(nc.scalar.copy, o_bf[:, :, 0:2], pair[:])
+                nc.vector.tensor_tensor(mixed[:].rearrange("p t v -> p (t v)"), low[:], capped[:], MAX)
+                for t in range(2):
+                    nc.sync.dma_start(out=out_mixed[t], in_=mixed[sides[t], :, :])
+                for b in range(2):
+                    regroup(b)
             else:
+                nc.vector.tensor_tensor(straight[:].rearrange("p t v -> p (t v)")[:, span(n)], low[:], capped[:], MAX)
                 for t, vs in groups[n]:
-                    nc.sync.dma_start(out=out_rows[:, t, vs], in_=pair[:, t % 2, vs])
+                    nc.sync.dma_start(out=out_rows[:, t, vs], in_=straight[:, t % 2, vs])
                 t, vs = groups[n][-1]
                 if t == PACK - 1:
-                    weave(nc.vector.tensor_copy if vs.stop == V else nc.scalar.copy, o_bf[:, vs, 2:4], pair[:, :, vs])
+                    weave(nc.vector.tensor_copy if vs.stop == V else nc.scalar.copy, o_bf[:, vs, 2:4], straight[:, :, vs])
 
         def hand_on(vs):
             nc.vector.quantize_mx(
@@ -172,7 +196,7 @@ def tile_picked_median_none_lo_kernel(
         for n, group in enumerate(groups):
             width = span(n).stop - span(n).start
             got = [sb.tile([P, width], F32, name="got%d_%d" % (n, i)) for i in range(3)]
-            steps = [(i, k) for k in reversed(range(len(group))) for i in range(3)]
+            steps = [(i, k) for k in range(len(group)) for i in range(3)]
             fetch(n, got, *steps[0])
             if pending is not None:
                 close(*pending)

@@ -22,6 +22,7 @@ LIST = 16
 HALF_N = N // 2
 HALF_P = P // 2
 EARLY = 320
+LAST = 64
 HALF_S = S // 2
 HALF_V = V // 2
 
@@ -136,23 +137,12 @@ def tile_picked_median_none_lo_kernel(
         o_codes = sb.tile([P, V], U32, name="o_codes", align_bytes=64)
         o_scales = sb.tile([P, V], U8, name="o_scales", align_bytes=64)
 
-        groups = [
-            [(0, slice(0, V)), (1, slice(0, V))],
-            [(2, slice(0, V))],
-            [(3, slice(0, HALF_V))],
-            [(3, slice(HALF_V, V))],
-        ]
-
-        def span(n):
-            t0, vs0 = groups[n][0]
-            t1, vs1 = groups[n][-1]
-            return slice((t0 % 2) * V + vs0.start, (t1 % 2) * V + vs1.stop)
+        groups = [(0, slice(0, V)), (2, slice(0, V - LAST)), (2, slice(V - LAST, V))]
 
         def fetch(n, got, i, k):
-            t, vs = groups[n][k]
-            first = (t % 2) * V - span(n).start
+            t, vs = groups[n]
             cols = slice(vs.start // LIST, vs.stop // LIST)
-            nc.vector.tensor_copy(got[i][:, first + vs.start : first + vs.stop], y[t][:].indirect(places[i][:, cols]))
+            nc.vector.tensor_copy(got[i][:, k, :], y[t + k][:].indirect(places[i][:, cols]))
 
         def regroup(b):
             vs = slice(b * HALF_V, (b + 1) * HALF_V)
@@ -170,19 +160,27 @@ def tile_picked_median_none_lo_kernel(
             weave(nc.scalar.copy, o_bf[:, vs, 0:2], back[:])
 
         def close(n, low, capped):
+            vs = groups[n][1]
             if n == 0:
-                nc.vector.tensor_tensor(mixed[:].rearrange("p t v -> p (t v)"), low[:], capped[:], MAX)
+                nc.vector.tensor_tensor(mixed[:], low[:], capped[:], MAX)
                 for t in range(2):
                     nc.sync.dma_start(out=out_mixed[t], in_=mixed[sides[t], :, :])
                 for b in range(2):
                     regroup(b)
             else:
-                nc.vector.tensor_tensor(straight[:].rearrange("p t v -> p (t v)")[:, span(n)], low[:], capped[:], MAX)
-                for t, vs in groups[n]:
-                    nc.sync.dma_start(out=out_rows[:, t, vs], in_=straight[:, t % 2, vs])
-                t, vs = groups[n][-1]
-                if t == PACK - 1:
-                    weave(nc.vector.tensor_copy if vs.stop == V else nc.scalar.copy, o_bf[:, vs, 2:4], straight[:, :, vs])
+                if n == 2:
+                    walk = "p e (c i) -> p c e i"
+                    nc.vector.tensor_tensor(
+                        o_bf[:, vs, 2:4].rearrange("p (c i) e -> p c e i", i=4),
+                        low[:].rearrange(walk, i=4),
+                        capped[:].rearrange(walk, i=4),
+                        MAX,
+                    )
+                nc.vector.tensor_tensor(straight[:, :, vs], low[:], capped[:], MAX)
+                nc.sync.dma_start(out=out_rows[:, 2:4, vs], in_=straight[:, :, vs])
+                if n == 1:
+                    for part, engine_copy in ((slice(0, HALF_V), nc.scalar.copy), (slice(HALF_V, V - LAST), nc.vector.tensor_copy)):
+                        weave(engine_copy, o_bf[:, part, 2:4], straight[:, :, part])
 
         def hand_on(vs):
             nc.vector.quantize_mx(
@@ -190,28 +188,30 @@ def tile_picked_median_none_lo_kernel(
                 scales=o_scales[:, vs],
                 in_=o_bf[:, vs, :].rearrange("p v t -> p (v t)"),
             )
-            nc.scalar.dma_start(out=out_words[:, vs], in_=o_codes[:, vs].bitcast(I32))
 
         pending = None
-        for n, group in enumerate(groups):
-            width = span(n).stop - span(n).start
-            got = [sb.tile([P, width], F32, name="got%d_%d" % (n, i)) for i in range(3)]
-            steps = [(i, k) for k in range(len(group)) for i in range(3)]
+        for n, (t, vs) in enumerate(groups):
+            shape = [P, 2, vs.stop - vs.start]
+            got = [sb.tile(shape, F32, name="got%d_%d" % (n, i)) for i in range(3)]
+            steps = [(i, k) for k in range(2) for i in range(3)]
             fetch(n, got, *steps[0])
             if pending is not None:
                 close(*pending)
             for i, k in steps[1:]:
                 fetch(n, got, i, k)
-            high = sb.tile([P, width], F32, name="high%d" % n)
-            low = sb.tile([P, width], F32, name="low%d" % n)
-            capped = sb.tile([P, width], F32, name="capped%d" % n)
+            high = sb.tile(shape, F32, name="high%d" % n)
+            low = sb.tile(shape, F32, name="low%d" % n)
+            capped = sb.tile(shape, F32, name="capped%d" % n)
             nc.vector.tensor_tensor(high[:], got[0][:], got[1][:], MAX)
             nc.vector.tensor_tensor(low[:], got[0][:], got[1][:], MIN)
             nc.vector.tensor_tensor(capped[:], high[:], got[2][:], MIN)
             pending = (n, low, capped)
         hand_on(slice(0, HALF_V))
+        hand_on(slice(HALF_V, V - LAST))
+        nc.scalar.dma_start(out=out_words[:, 0 : V - LAST], in_=o_codes[:, 0 : V - LAST].bitcast(I32))
         close(*pending)
-        hand_on(slice(HALF_V, V))
+        hand_on(slice(V - LAST, V))
+        nc.scalar.dma_start(out=out_words[:, V - LAST : V], in_=o_codes[:, V - LAST : V].bitcast(I32))
 
         scale_rows = o_scales[:].bitcast(I32)
         for q in range(4):

@@ -22,7 +22,7 @@ LIST = 16
 HALF_N = N // 2
 HALF_P = P // 2
 EARLY = 320
-LAST = 64
+SCALAR_SHARE = 128
 HALF_S = S // 2
 HALF_V = V // 2
 
@@ -56,7 +56,7 @@ def tile_picked_median_none_lo_kernel(
             nc.sync.dma_start(place[:], pos)
             places.append(place)
 
-        pairs = [sb.tile([P, 2, S], F32, name="x_pair%d" % u) for u in range(2)]
+        planes = sb.tile([P, PACK, S], F32, name="planes")
         rounded = sb.tile([P, (S + N) * PACK], BF16, name="rounded", align_bytes=64)
         codes = sb.tile([P, S + N], U32, name="codes", align_bytes=64)
         scales = sb.tile([P, S + N], U8, name="scales", align_bytes=64)
@@ -71,14 +71,16 @@ def tile_picked_median_none_lo_kernel(
                 in_=src.rearrange("p e (c i) -> p c e i", i=4),
             )
 
-        parts = [slice(0, EARLY), slice(EARLY, S)]
-        for u, engine_copy in enumerate((nc.scalar.copy, nc.vector.tensor_copy)):
-            nc.vector.tensor_copy(pairs[u][:, 0, :], x_raw[2 * u][:].indirect(picked[:]))
-            for part in parts:
-                cols = slice(part.start // LIST, part.stop // LIST)
-                nc.vector.tensor_copy(pairs[u][:, 1, part], x_raw[2 * u + 1][:].indirect(picked[:, cols]))
-            for part in parts:
-                weave(engine_copy, x_bf[:, part, 2 * u : 2 * u + 2], pairs[u][:, :, part])
+        for j in range(PACK):
+            cuts = ((0, S), (0, EARLY, S), (0, S), (0, SCALAR_SHARE, EARLY, S))[j]
+            for first, stop in zip(cuts, cuts[1:]):
+                nc.vector.tensor_copy(planes[:, j, first:stop], x_raw[j][:].indirect(picked[:, first // LIST : stop // LIST]))
+            if j == 1:
+                for part in (slice(SCALAR_SHARE, EARLY), slice(EARLY, S)):
+                    weave(nc.scalar.copy, x_bf[:, part, 0:2], planes[:, 0:2, part])
+        weave(nc.scalar.copy, x_bf[:, 0:SCALAR_SHARE, :], planes[:, :, 0:SCALAR_SHARE])
+        for part in (slice(SCALAR_SHARE, EARLY), slice(EARLY, S)):
+            weave(nc.vector.tensor_copy, x_bf[:, part, 2:4], planes[:, 2:4, part])
 
         def quantize(first, stop):
             nc.vector.quantize_mx(
@@ -137,12 +139,23 @@ def tile_picked_median_none_lo_kernel(
         o_codes = sb.tile([P, V], U32, name="o_codes", align_bytes=64)
         o_scales = sb.tile([P, V], U8, name="o_scales", align_bytes=64)
 
-        groups = [(0, slice(0, V)), (2, slice(0, V - LAST)), (2, slice(V - LAST, V))]
+        groups = [
+            [(0, slice(0, V)), (1, slice(0, V))],
+            [(2, slice(0, V))],
+            [(3, slice(0, HALF_V))],
+            [(3, slice(HALF_V, V))],
+        ]
+
+        def span(n):
+            t0, vs0 = groups[n][0]
+            t1, vs1 = groups[n][-1]
+            return slice((t0 % 2) * V + vs0.start, (t1 % 2) * V + vs1.stop)
 
         def fetch(n, got, i, k):
-            t, vs = groups[n]
+            t, vs = groups[n][k]
+            first = (t % 2) * V - span(n).start
             cols = slice(vs.start // LIST, vs.stop // LIST)
-            nc.vector.tensor_copy(got[i][:, k, :], y[t + k][:].indirect(places[i][:, cols]))
+            nc.vector.tensor_copy(got[i][:, first + vs.start : first + vs.stop], y[t][:].indirect(places[i][:, cols]))
 
         def regroup(b):
             vs = slice(b * HALF_V, (b + 1) * HALF_V)
@@ -160,27 +173,19 @@ def tile_picked_median_none_lo_kernel(
             weave(nc.scalar.copy, o_bf[:, vs, 0:2], back[:])
 
         def close(n, low, capped):
-            vs = groups[n][1]
             if n == 0:
-                nc.vector.tensor_tensor(mixed[:], low[:], capped[:], MAX)
+                nc.vector.tensor_tensor(mixed[:].rearrange("p t v -> p (t v)"), low[:], capped[:], MAX)
                 for t in range(2):
                     nc.sync.dma_start(out=out_mixed[t], in_=mixed[sides[t], :, :])
                 for b in range(2):
                     regroup(b)
             else:
-                if n == 2:
-                    walk = "p e (c i) -> p c e i"
-                    nc.vector.tensor_tensor(
-                        o_bf[:, vs, 2:4].rearrange("p (c i) e -> p c e i", i=4),
-                        low[:].rearrange(walk, i=4),
-                        capped[:].rearrange(walk, i=4),
-                        MAX,
-                    )
-                nc.vector.tensor_tensor(straight[:, :, vs], low[:], capped[:], MAX)
-                nc.sync.dma_start(out=out_rows[:, 2:4, vs], in_=straight[:, :, vs])
-                if n == 1:
-                    for part, engine_copy in ((slice(0, HALF_V), nc.scalar.copy), (slice(HALF_V, V - LAST), nc.vector.tensor_copy)):
-                        weave(engine_copy, o_bf[:, part, 2:4], straight[:, :, part])
+                nc.vector.tensor_tensor(straight[:].rearrange("p t v -> p (t v)")[:, span(n)], low[:], capped[:], MAX)
+                for t, vs in groups[n]:
+                    nc.sync.dma_start(out=out_rows[:, t, vs], in_=straight[:, t % 2, vs])
+                t, vs = groups[n][-1]
+                if t == PACK - 1:
+                    weave(nc.vector.tensor_copy if vs.stop == V else nc.scalar.copy, o_bf[:, vs, 2:4], straight[:, :, vs])
 
         def hand_on(vs):
             nc.vector.quantize_mx(
@@ -188,30 +193,28 @@ def tile_picked_median_none_lo_kernel(
                 scales=o_scales[:, vs],
                 in_=o_bf[:, vs, :].rearrange("p v t -> p (v t)"),
             )
+            nc.scalar.dma_start(out=out_words[:, vs], in_=o_codes[:, vs].bitcast(I32))
 
         pending = None
-        for n, (t, vs) in enumerate(groups):
-            shape = [P, 2, vs.stop - vs.start]
-            got = [sb.tile(shape, F32, name="got%d_%d" % (n, i)) for i in range(3)]
-            steps = [(i, k) for k in range(2) for i in range(3)]
+        for n, group in enumerate(groups):
+            width = span(n).stop - span(n).start
+            got = [sb.tile([P, width], F32, name="got%d_%d" % (n, i)) for i in range(3)]
+            steps = [(i, k) for k in range(len(group)) for i in range(3)]
             fetch(n, got, *steps[0])
             if pending is not None:
                 close(*pending)
             for i, k in steps[1:]:
                 fetch(n, got, i, k)
-            high = sb.tile(shape, F32, name="high%d" % n)
-            low = sb.tile(shape, F32, name="low%d" % n)
-            capped = sb.tile(shape, F32, name="capped%d" % n)
+            high = sb.tile([P, width], F32, name="high%d" % n)
+            low = sb.tile([P, width], F32, name="low%d" % n)
+            capped = sb.tile([P, width], F32, name="capped%d" % n)
             nc.vector.tensor_tensor(high[:], got[0][:], got[1][:], MAX)
             nc.vector.tensor_tensor(low[:], got[0][:], got[1][:], MIN)
             nc.vector.tensor_tensor(capped[:], high[:], got[2][:], MIN)
             pending = (n, low, capped)
         hand_on(slice(0, HALF_V))
-        hand_on(slice(HALF_V, V - LAST))
-        nc.scalar.dma_start(out=out_words[:, 0 : V - LAST], in_=o_codes[:, 0 : V - LAST].bitcast(I32))
         close(*pending)
-        hand_on(slice(V - LAST, V))
-        nc.scalar.dma_start(out=out_words[:, V - LAST : V], in_=o_codes[:, V - LAST : V].bitcast(I32))
+        hand_on(slice(HALF_V, V))
 
         scale_rows = o_scales[:].bitcast(I32)
         for q in range(4):

@@ -15,16 +15,21 @@ U8 = mybir.dt.uint8
 FP8X4 = mybir.dt.float8_e4m3fn_x4
 MAX = mybir.AluOpType.max
 MIN = mybir.AluOpType.min
+COPY = mybir.ActivationFunctionType.Copy
 
 P = 128
 PACK = 4
 LIST = 16
+RUN = 4
+QUADRANT = 32
+SCALE_ROWS = 4
 HALF_N = N // 2
 HALF_P = P // 2
-EARLY = 320
-SCALAR_SHARE = 128
 HALF_S = S // 2
 HALF_V = V // 2
+EARLY = S + HALF_P - 2 * P
+SCALAR_SHARE = 128
+SCALAR_LOOKUPS = 128
 
 
 def tile_picked_median_none_lo_kernel(
@@ -56,7 +61,13 @@ def tile_picked_median_none_lo_kernel(
             nc.sync.dma_start(place[:], pos)
             places.append(place)
 
-        planes = sb.tile([P, PACK, S], F32, name="planes")
+        x_picked = sb.tile([P, PACK, S], BF16, name="x_picked")
+        x0_bf = sb.tile([P, T], BF16, name="x0_bf")
+        nc.scalar.copy(out=x0_bf[:], in_=x_raw[0][:])
+        nc.scalar.activation(
+            x_picked[:, 0, S - SCALAR_LOOKUPS : S], x0_bf[:].indirect(picked[:, (S - SCALAR_LOOKUPS) // LIST :]), COPY
+        )
+
         rounded = sb.tile([P, (S + N) * PACK], BF16, name="rounded", align_bytes=64)
         codes = sb.tile([P, S + N], U32, name="codes", align_bytes=64)
         scales = sb.tile([P, S + N], U8, name="scales", align_bytes=64)
@@ -67,20 +78,22 @@ def tile_picked_median_none_lo_kernel(
 
         def weave(engine_copy, dst, src):
             engine_copy(
-                out=dst.rearrange("p (c i) e -> p c e i", i=4),
-                in_=src.rearrange("p e (c i) -> p c e i", i=4),
+                out=dst.rearrange("p (c i) e -> p c e i", i=RUN),
+                in_=src.rearrange("p e (c i) -> p c e i", i=RUN),
             )
 
+        lookup_cuts = ((0, S - SCALAR_LOOKUPS), (0, EARLY, S), (0, S), (0, SCALAR_SHARE, EARLY, S))
         for j in range(PACK):
-            cuts = ((0, S), (0, EARLY, S), (0, S), (0, SCALAR_SHARE, EARLY, S))[j]
-            for first, stop in zip(cuts, cuts[1:]):
-                nc.vector.tensor_copy(planes[:, j, first:stop], x_raw[j][:].indirect(picked[:, first // LIST : stop // LIST]))
+            for first, stop in zip(lookup_cuts[j], lookup_cuts[j][1:]):
+                nc.vector.tensor_copy(
+                    x_picked[:, j, first:stop], x_raw[j][:].indirect(picked[:, first // LIST : stop // LIST])
+                )
             if j == 1:
                 for part in (slice(SCALAR_SHARE, EARLY), slice(EARLY, S)):
-                    weave(nc.scalar.copy, x_bf[:, part, 0:2], planes[:, 0:2, part])
-        weave(nc.scalar.copy, x_bf[:, 0:SCALAR_SHARE, :], planes[:, :, 0:SCALAR_SHARE])
+                    weave(nc.scalar.copy, x_bf[:, part, 0:2], x_picked[:, 0:2, part])
+        weave(nc.scalar.copy, x_bf[:, 0:SCALAR_SHARE, :], x_picked[:, :, 0:SCALAR_SHARE])
         for part in (slice(SCALAR_SHARE, EARLY), slice(EARLY, S)):
-            weave(nc.vector.tensor_copy, x_bf[:, part, 2:4], planes[:, 2:4, part])
+            weave(nc.vector.tensor_copy, x_bf[:, part, 2:4], x_picked[:, 2:4, part])
 
         def quantize(first, stop):
             nc.vector.quantize_mx(
@@ -95,11 +108,11 @@ def tile_picked_median_none_lo_kernel(
                 in_=w_raw[h][:].rearrange("p j (m t) -> p m j t", t=PACK)[:, :, :, ts],
             )
 
-        y = [sb.tile([P, S], F32, name="y%d" % t) for t in range(PACK)]
+        y = [sb.tile([P, S], F32, name="y%d" % tile) for tile in range(PACK)]
 
-        def product(name, t, cols, engine_copy):
-            acc = ps.tile([P, cols.stop - cols.start], F32, name=name, tag=name)
-            w_cols = slice(first_col[t], first_col[t] + P)
+        def product(bank, tile, cols, engine_copy):
+            acc = ps.tile([P, cols.stop - cols.start], F32, name=bank, tag=bank)
+            w_cols = slice(first_col[tile], first_col[tile] + P)
             nc.tensor.matmul_mx(
                 out=acc[:],
                 lhsT=codes[:, w_cols].bitcast(FP8X4),
@@ -109,7 +122,7 @@ def tile_picked_median_none_lo_kernel(
                 start=True,
                 stop=True,
             )
-            engine_copy(out=y[t][:, cols], in_=acc[:])
+            engine_copy(out=y[tile][:, cols], in_=acc[:])
 
         quantize(0, HALF_P)
         quantize(HALF_P, EARLY)
@@ -125,9 +138,9 @@ def tile_picked_median_none_lo_kernel(
         quantize(first_col[1], first_col[1] + P)
         product("acc1", 1, slice(0, S), nc.scalar.copy)
         deal(w_straight[:, :, HALF_P:P, :], 1, slice(2, PACK))
-        for t in (2, 3):
-            quantize(first_col[t] + HALF_P, first_col[t] + P)
-            product("acc%d" % t, t, slice(0, S), nc.scalar.copy)
+        for tile in (2, 3):
+            quantize(first_col[tile] + HALF_P, first_col[tile] + P)
+            product("acc%d" % tile, tile, slice(0, S), nc.scalar.copy)
 
         identity = sb.tile([P, P], F32, name="identity")
         make_identity(nc, identity[:])
@@ -147,19 +160,21 @@ def tile_picked_median_none_lo_kernel(
         ]
 
         def span(n):
-            t0, vs0 = groups[n][0]
-            t1, vs1 = groups[n][-1]
-            return slice((t0 % 2) * V + vs0.start, (t1 % 2) * V + vs1.stop)
+            tile0, vs0 = groups[n][0]
+            tile1, vs1 = groups[n][-1]
+            return slice((tile0 % 2) * V + vs0.start, (tile1 % 2) * V + vs1.stop)
 
-        def fetch(n, got, i, k):
-            t, vs = groups[n][k]
-            first = (t % 2) * V - span(n).start
+        def fetch(n, got, i, member):
+            tile, vs = groups[n][member]
+            first = (tile % 2) * V - span(n).start
             cols = slice(vs.start // LIST, vs.stop // LIST)
-            nc.vector.tensor_copy(got[i][:, first + vs.start : first + vs.stop], y[t][:].indirect(places[i][:, cols]))
+            nc.vector.tensor_copy(
+                got[i][:, first + vs.start : first + vs.stop], y[tile][:].indirect(places[i][:, cols])
+            )
 
         def regroup(b):
             vs = slice(b * HALF_V, (b + 1) * HALF_V)
-            across = ps.tile([P, 2, P], F32, name="across%d" % b, tag="acc0%s" % "ab"[b])
+            across = ps.tile([P, 2, P], F32, name="across%d" % b, tag=("acc0a", "acc0b")[b])
             for h in range(2):
                 nc.tensor.transpose(across[:, h, :], mixed[:, h, vs], identity[:])
             turned = sb.tile([P, 2, P], F32, name="turned%d" % b)
@@ -174,18 +189,18 @@ def tile_picked_median_none_lo_kernel(
 
         def close(n, low, capped):
             if n == 0:
-                nc.vector.tensor_tensor(mixed[:].rearrange("p t v -> p (t v)"), low[:], capped[:], MAX)
+                nc.vector.tensor_tensor(mixed[:].rearrange("p h v -> p (h v)"), low[:], capped[:], MAX)
                 for t in range(2):
                     nc.sync.dma_start(out=out_mixed[t], in_=mixed[sides[t], :, :])
                 for b in range(2):
                     regroup(b)
             else:
                 nc.vector.tensor_tensor(straight[:].rearrange("p t v -> p (t v)")[:, span(n)], low[:], capped[:], MAX)
-                for t, vs in groups[n]:
-                    nc.sync.dma_start(out=out_rows[:, t, vs], in_=straight[:, t % 2, vs])
-                t, vs = groups[n][-1]
-                if t == PACK - 1:
-                    weave(nc.vector.tensor_copy if vs.stop == V else nc.scalar.copy, o_bf[:, vs, 2:4], straight[:, :, vs])
+                [(tile, vs)] = groups[n]
+                nc.sync.dma_start(out=out_rows[:, tile, vs], in_=straight[:, tile % 2, vs])
+                if tile == PACK - 1:
+                    engine_copy = nc.vector.tensor_copy if n == len(groups) - 1 else nc.scalar.copy
+                    weave(engine_copy, o_bf[:, vs, 2:4], straight[:, :, vs])
 
         def hand_on(vs):
             nc.vector.quantize_mx(
@@ -199,12 +214,12 @@ def tile_picked_median_none_lo_kernel(
         for n, group in enumerate(groups):
             width = span(n).stop - span(n).start
             got = [sb.tile([P, width], F32, name="got%d_%d" % (n, i)) for i in range(3)]
-            steps = [(i, k) for k in range(len(group)) for i in range(3)]
+            steps = [(i, member) for member in range(len(group)) for i in range(3)]
             fetch(n, got, *steps[0])
             if pending is not None:
                 close(*pending)
-            for i, k in steps[1:]:
-                fetch(n, got, i, k)
+            for i, member in steps[1:]:
+                fetch(n, got, i, member)
             high = sb.tile([P, width], F32, name="high%d" % n)
             low = sb.tile([P, width], F32, name="low%d" % n)
             capped = sb.tile([P, width], F32, name="capped%d" % n)
@@ -217,6 +232,9 @@ def tile_picked_median_none_lo_kernel(
         hand_on(slice(HALF_V, V))
 
         scale_rows = o_scales[:].bitcast(I32)
-        for q in range(4):
+        for q in range(P // QUADRANT):
             queue = nc.sync if q % 2 == 0 else nc.scalar
-            queue.dma_start(out=out_scales[4 * q : 4 * q + 4, :], in_=scale_rows[32 * q : 32 * q + 4, :])
+            queue.dma_start(
+                out=out_scales[SCALE_ROWS * q : SCALE_ROWS * (q + 1), :],
+                in_=scale_rows[QUADRANT * q : QUADRANT * q + SCALE_ROWS, :],
+            )

@@ -1,7 +1,6 @@
 from contextlib import ExitStack
 
 import concourse.mybir as mybir
-from concourse.masks import make_identity
 
 K, T, S, V, N = 512, 1024, 512, 256, 512
 FLOPS = 2 * K * N * S
@@ -27,9 +26,8 @@ HALF_N = N // 2
 HALF_P = P // 2
 HALF_S = S // 2
 HALF_V = V // 2
-EARLY = S + HALF_P - 2 * P
-SCALAR_SHARE = 128
-SCALAR_LOOKUPS = 128
+VECTOR_WEAVES = 384
+VECTOR_DEALS = 40
 
 
 def tile_picked_median_none_lo_kernel(
@@ -47,71 +45,93 @@ def tile_picked_median_none_lo_kernel(
         out_scales = out_2[0].bitcast(I32)
 
         x_raw = [sb.tile([P, T], F32, name="x_raw%d" % j) for j in range(PACK)]
+        w_first = sb.tile([P, HALF_N], F32, name="w_first")
+        w_rest = sb.tile([P, PACK - 1, HALF_N], F32, name="w_rest")
+        w_last = sb.tile([P, PACK, HALF_N], F32, name="w_last")
         picked = sb.tile([P, S // LIST], U16, name="picked")
-        nc.sync.dma_start(out=x_raw[0][:], in_=x_rows[:, 0, :])
+        nc.sync.dma_start(out=w_first[:], in_=w_rows[:, 0, 0:HALF_N])
         nc.sync.dma_start(picked[:], offs)
-        for j in range(1, PACK):
+        for j in range(PACK):
             nc.sync.dma_start(out=x_raw[j][:], in_=x_rows[:, j, :])
-        w_raw = [sb.tile([P, PACK, HALF_N], F32, name="w_raw%d" % h) for h in range(2)]
-        for h in range(2):
-            nc.sync.dma_start(out=w_raw[h][:], in_=w_rows[:, :, h * HALF_N : (h + 1) * HALF_N])
+        nc.sync.dma_start(out=w_rest[:], in_=w_rows[:, 1:PACK, 0:HALF_N])
+        nc.sync.dma_start(out=w_last[:], in_=w_rows[:, :, HALF_N:N])
         places = []
         for i, pos in enumerate((pos1, pos2, pos3)):
             place = sb.tile([P, V // LIST], U16, name="place%d" % i)
             nc.sync.dma_start(place[:], pos)
             places.append(place)
 
-        x_picked = sb.tile([P, PACK, S], BF16, name="x_picked")
-        x0_bf = sb.tile([P, T], BF16, name="x0_bf")
-        nc.scalar.copy(out=x0_bf[:], in_=x_raw[0][:])
-        nc.scalar.activation(
-            x_picked[:, 0, S - SCALAR_LOOKUPS : S], x0_bf[:].indirect(picked[:, (S - SCALAR_LOOKUPS) // LIST :]), COPY
-        )
+        def vector_lookup(dst, src):
+            nc.vector.tensor_copy(dst, src)
 
+        def scalar_lookup(dst, src):
+            nc.scalar.activation(dst, src, COPY)
+
+        x_picked = sb.tile([P, PACK, S], BF16, name="x_picked")
         rounded = sb.tile([P, (S + N) * PACK], BF16, name="rounded", align_bytes=64)
         codes = sb.tile([P, S + N], U32, name="codes", align_bytes=64)
         scales = sb.tile([P, S + N], U8, name="scales", align_bytes=64)
         x_bf = rounded[:, 0 : S * PACK].rearrange("p (s j) -> p s j", j=PACK)
-        first_col = {2: S, 3: S + P, 0: S + 2 * P, 1: S + 3 * P}
-        w_straight = rounded[:, S * PACK : (S + 2 * P) * PACK].rearrange("p (t m j) -> p t m j", t=2, j=PACK)
-        w_mixed = rounded[:, (S + 2 * P) * PACK :].rearrange("p (h t m j) -> p h t m j", h=2, t=2, j=PACK)
+        w_bf = rounded[:, S * PACK :].rearrange("p (t m j) -> p t m j", t=PACK, j=PACK)
+        first_col = [S + tile * P for tile in range(PACK)]
+
+        def by_runs_woven(ap):
+            return ap.rearrange("p (c i) e -> p c e i", i=RUN)
+
+        def by_runs_apart(ap):
+            return ap.rearrange("p e (c i) -> p c e i", i=RUN)
 
         def weave(engine_copy, dst, src):
-            engine_copy(
-                out=dst.rearrange("p (c i) e -> p c e i", i=RUN),
-                in_=src.rearrange("p e (c i) -> p c e i", i=RUN),
-            )
+            engine_copy(out=by_runs_woven(dst), in_=by_runs_apart(src))
 
-        lookup_cuts = ((0, S - SCALAR_LOOKUPS), (0, EARLY, S), (0, S), (0, SCALAR_SHARE, EARLY, S))
-        for j in range(PACK):
-            for first, stop in zip(lookup_cuts[j], lookup_cuts[j][1:]):
-                nc.vector.tensor_copy(
-                    x_picked[:, j, first:stop], x_raw[j][:].indirect(picked[:, first // LIST : stop // LIST])
-                )
-            if j == 1:
-                for part in (slice(SCALAR_SHARE, EARLY), slice(EARLY, S)):
-                    weave(nc.scalar.copy, x_bf[:, part, 0:2], x_picked[:, 0:2, part])
-        weave(nc.scalar.copy, x_bf[:, 0:SCALAR_SHARE, :], x_picked[:, :, 0:SCALAR_SHARE])
-        for part in (slice(SCALAR_SHARE, EARLY), slice(EARLY, S)):
-            weave(nc.vector.tensor_copy, x_bf[:, part, 2:4], x_picked[:, 2:4, part])
-
-        def quantize(first, stop):
+        def quantize(words, scale_bytes, values, first, stop):
             nc.vector.quantize_mx(
-                out=codes[:, first:stop].bitcast(FP8X4),
-                scales=scales[:, first:stop],
-                in_=rounded[:, first * PACK : stop * PACK],
+                out=words[:, first:stop].bitcast(FP8X4),
+                scales=scale_bytes[:, first:stop],
+                in_=values[:, first * PACK : stop * PACK],
             )
 
-        def deal(dst, h, ts):
-            nc.scalar.copy(
-                out=dst.rearrange("p t m j -> p m j t"),
-                in_=w_raw[h][:].rearrange("p j (m t) -> p m j t", t=PACK)[:, :, :, ts],
+        def pick(lookup, j, cols):
+            lookup(x_picked[:, j, cols], x_raw[j][:].indirect(picked[:, cols.start // LIST : cols.stop // LIST]))
+
+        def weave_pair(engine_copy, j, cols):
+            weave(engine_copy, x_bf[:, cols, j : j + 2], x_picked[:, j : j + 2, cols])
+
+        def deal_last(engine_copy, ms, ts):
+            engine_copy(
+                out=w_bf[:, ts, HALF_P + ms.start : HALF_P + ms.stop, :].rearrange("p t m j -> p m j t"),
+                in_=w_last[:].rearrange("p j (m t) -> p m j t", t=PACK)[:, ms, :, ts],
             )
 
-        y = [sb.tile([P, S], F32, name="y%d" % tile) for tile in range(PACK)]
+        nc.scalar.copy(
+            out=w_bf[:, :, 0:HALF_P, 0].rearrange("p t m -> p m t"),
+            in_=w_first[:].rearrange("p (m t) -> p m t", t=PACK),
+        )
+        for j in range(PACK):
+            pick(vector_lookup, j, slice(0, HALF_S))
+            pick(scalar_lookup, j, slice(HALF_S, S))
+            if j % 2 == 1:
+                weave_pair(nc.vector.tensor_copy, j - 1, slice(0, HALF_S))
+                weave_pair(nc.vector.tensor_copy, j - 1, slice(HALF_S, VECTOR_WEAVES))
+                weave_pair(nc.scalar.copy, j - 1, slice(VECTOR_WEAVES, S))
+        quantize(codes, scales, rounded, 0, HALF_S)
+        quantize(codes, scales, rounded, HALF_S, S - P)
+        nc.scalar.copy(
+            out=w_bf[:, :, 0:HALF_P, 1:PACK].rearrange("p t m j -> p m j t"),
+            in_=w_rest[:].rearrange("p j (m t) -> p m j t", t=PACK),
+        )
+        early, late = slice(0, 2), slice(2, PACK)
+        deal_last(nc.vector.tensor_copy, slice(0, VECTOR_DEALS), early)
+        deal_last(nc.scalar.copy, slice(VECTOR_DEALS, HALF_P), early)
+        quantize(codes, scales, rounded, first_col[1], first_col[1] + P)
+        quantize(codes, scales, rounded, S - P, first_col[0] + P)
+        deal_last(nc.scalar.copy, slice(0, HALF_P), late)
+        quantize(codes, scales, rounded, first_col[2], first_col[3] + P)
 
-        def product(bank, tile, cols, engine_copy):
-            acc = ps.tile([P, cols.stop - cols.start], F32, name=bank, tag=bank)
+        y = [sb.tile([P, S], F32, name="y%d" % tile, tag="y%d" % (tile % 3)) for tile in range(PACK)]
+
+        def product(bank, tile, cols):
+            acc = ps.tile([P, cols.stop - cols.start], F32, name=bank)
             w_cols = slice(first_col[tile], first_col[tile] + P)
             nc.tensor.matmul_mx(
                 out=acc[:],
@@ -122,114 +142,89 @@ def tile_picked_median_none_lo_kernel(
                 start=True,
                 stop=True,
             )
-            engine_copy(out=y[tile][:, cols], in_=acc[:])
+            return acc
 
-        quantize(0, HALF_P)
-        quantize(HALF_P, EARLY)
-        deal(w_mixed[:, 0], 0, slice(0, 2))
-        quantize(first_col[0], first_col[0] + P)
-        deal(w_straight[:, :, 0:HALF_P, :], 0, slice(2, PACK))
-        quantize(EARLY, S + HALF_P)
-        product("acc0a", 0, slice(0, HALF_S), nc.vector.tensor_copy)
-        product("acc0b", 0, slice(HALF_S, S - P), nc.scalar.copy)
-        product("acc0c", 0, slice(S - P, S), nc.scalar.copy)
-        quantize(first_col[3], first_col[3] + HALF_P)
-        deal(w_mixed[:, 1], 1, slice(0, 2))
-        quantize(first_col[1], first_col[1] + P)
-        product("acc1", 1, slice(0, S), nc.scalar.copy)
-        deal(w_straight[:, :, HALF_P:P, :], 1, slice(2, PACK))
-        for tile in (2, 3):
-            quantize(first_col[tile] + HALF_P, first_col[tile] + P)
-            product("acc%d" % tile, tile, slice(0, S), nc.scalar.copy)
+        pieces = (slice(0, HALF_S), slice(HALF_S, S - P), slice(S - P, S))
+        first_banks = [product("acc1%d" % b, 1, pieces[b]) for b in range(len(pieces))]
+        banks = {tile: product("acc%d" % tile, tile, slice(0, S)) for tile in (0, 2, 3)}
 
-        identity = sb.tile([P, P], F32, name="identity")
-        make_identity(nc, identity[:])
-        mixed = sb.tile([P, 2, V], F32, name="mixed")
-        straight = sb.tile([P, 2, V], F32, name="straight")
-        out_mixed = out_0.rearrange("(h m t) v -> t m h v", h=2, t=PACK)
-        sides = [slice(0, HALF_P), slice(HALF_P, P)]
+        high = sb.tile([P, PACK, V], F32, name="high")
+        low = sb.tile([P, PACK, V], F32, name="low")
+        capped = sb.tile([P, PACK, V], F32, name="capped")
+        median = sb.tile([P, PACK, V], F32, name="median")
         o_bf = sb.tile([P, V, PACK], BF16, name="o_bf", align_bytes=64)
         o_codes = sb.tile([P, V], U32, name="o_codes", align_bytes=64)
         o_scales = sb.tile([P, V], U8, name="o_scales", align_bytes=64)
+        o_flat = o_bf[:].rearrange("p v t -> p (v t)")
+        whole, front, back = slice(0, V), slice(0, HALF_V), slice(HALF_V, V)
 
-        groups = [
-            [(0, slice(0, V)), (1, slice(0, V))],
-            [(2, slice(0, V))],
-            [(3, slice(0, HALF_V))],
-            [(3, slice(HALF_V, V))],
-        ]
+        def neighbours(name, tag, vs):
+            return [
+                sb.tile([P, 2, vs.stop - vs.start], F32, name="%s%d" % (name, i), tag="%s%d" % (tag, i))
+                for i in range(len(places))
+            ]
 
-        def span(n):
-            tile0, vs0 = groups[n][0]
-            tile1, vs1 = groups[n][-1]
-            return slice((tile0 % 2) * V + vs0.start, (tile1 % 2) * V + vs1.stop)
+        def fetch(lookup, got, i, tile, vs):
+            lookup(got[i][:, tile % 2, :], y[tile][:].indirect(places[i][:, vs.start // LIST : vs.stop // LIST]))
 
-        def fetch(n, got, i, member):
-            tile, vs = groups[n][member]
-            first = (tile % 2) * V - span(n).start
-            cols = slice(vs.start // LIST, vs.stop // LIST)
-            nc.vector.tensor_copy(
-                got[i][:, first + vs.start : first + vs.stop], y[tile][:].indirect(places[i][:, cols])
-            )
+        def bounds(got, ts, vs):
+            nc.vector.tensor_tensor(high[:, ts, vs], got[0][:], got[1][:], MAX)
+            nc.vector.tensor_tensor(low[:, ts, vs], got[0][:], got[1][:], MIN)
 
-        def regroup(b):
-            vs = slice(b * HALF_V, (b + 1) * HALF_V)
-            across = ps.tile([P, 2, P], F32, name="across%d" % b, tag=("acc0a", "acc0b")[b])
-            for h in range(2):
-                nc.tensor.transpose(across[:, h, :], mixed[:, h, vs], identity[:])
-            turned = sb.tile([P, 2, P], F32, name="turned%d" % b)
-            nc.scalar.copy(
-                out=turned[:].rearrange("p t (h m) -> p t h m", h=2),
-                in_=across[:].rearrange("p h (t m) -> p t h m", t=2),
-            )
-            back = ps.tile([P, 2, HALF_V], F32, name="back%d" % b)
-            for t in range(2):
-                nc.tensor.transpose(back[:, t, :], turned[:, t, :], identity[:])
-            weave(nc.scalar.copy, o_bf[:, vs, 0:2], back[:])
+        def cap(got, ts, vs):
+            nc.vector.tensor_tensor(capped[:, ts, vs], high[:, ts, vs], got[2][:], MIN)
 
-        def close(n, low, capped):
-            if n == 0:
-                nc.vector.tensor_tensor(mixed[:].rearrange("p h v -> p (h v)"), low[:], capped[:], MAX)
-                for t in range(2):
-                    nc.sync.dma_start(out=out_mixed[t], in_=mixed[sides[t], :, :])
-                for b in range(2):
-                    regroup(b)
-            else:
-                nc.vector.tensor_tensor(straight[:].rearrange("p t v -> p (t v)")[:, span(n)], low[:], capped[:], MAX)
-                [(tile, vs)] = groups[n]
-                nc.sync.dma_start(out=out_rows[:, tile, vs], in_=straight[:, tile % 2, vs])
-                if tile == PACK - 1:
-                    engine_copy = nc.vector.tensor_copy if n == len(groups) - 1 else nc.scalar.copy
-                    weave(engine_copy, o_bf[:, vs, 2:4], straight[:, :, vs])
+        def close(ts, vs):
+            nc.vector.tensor_tensor(median[:, ts, vs], low[:, ts, vs], capped[:, ts, vs], MAX)
+            nc.sync.dma_start(out=out_rows[:, ts, vs], in_=median[:, ts, vs])
 
         def hand_on(vs):
-            nc.vector.quantize_mx(
-                out=o_codes[:, vs].bitcast(FP8X4),
-                scales=o_scales[:, vs],
-                in_=o_bf[:, vs, :].rearrange("p v t -> p (v t)"),
-            )
+            quantize(o_codes, o_scales, o_flat, vs.start, vs.stop)
             nc.scalar.dma_start(out=out_words[:, vs], in_=o_codes[:, vs].bitcast(I32))
 
-        pending = None
-        for n, group in enumerate(groups):
-            width = span(n).stop - span(n).start
-            got = [sb.tile([P, width], F32, name="got%d_%d" % (n, i)) for i in range(3)]
-            steps = [(i, member) for member in range(len(group)) for i in range(3)]
-            fetch(n, got, *steps[0])
-            if pending is not None:
-                close(*pending)
-            for i, member in steps[1:]:
-                fetch(n, got, i, member)
-            high = sb.tile([P, width], F32, name="high%d" % n)
-            low = sb.tile([P, width], F32, name="low%d" % n)
-            capped = sb.tile([P, width], F32, name="capped%d" % n)
-            nc.vector.tensor_tensor(high[:], got[0][:], got[1][:], MAX)
-            nc.vector.tensor_tensor(low[:], got[0][:], got[1][:], MIN)
-            nc.vector.tensor_tensor(capped[:], high[:], got[2][:], MIN)
-            pending = (n, low, capped)
-        hand_on(slice(0, HALF_V))
-        close(*pending)
-        hand_on(slice(HALF_V, V))
+        for b, engine_copy in enumerate((nc.vector.tensor_copy, nc.scalar.copy, nc.scalar.copy)):
+            engine_copy(out=y[1][:, pieces[b]], in_=first_banks[b][:])
+        got_early = neighbours("got_early", "wide", whole)
+        for i in range(2):
+            fetch(scalar_lookup, got_early, i, 1, whole)
+        nc.vector.tensor_copy(out=y[0][:], in_=banks[0][:])
+        fetch(vector_lookup, got_early, 2, 1, whole)
+        for i in range(2):
+            fetch(scalar_lookup, got_early, i, 0, whole)
+        fetch(vector_lookup, got_early, 2, 0, whole)
+        nc.vector.tensor_copy(out=y[2][:], in_=banks[2][:])
+        nc.scalar.copy(out=y[3][:], in_=banks[3][:])
+
+        got_front = neighbours("got_front", "narrow", front)
+        for i in range(2):
+            for tile in (2, 3):
+                fetch(scalar_lookup, got_front, i, tile, front)
+        bounds(got_early, early, whole)
+        cap(got_early, early, whole)
+        fetch(vector_lookup, got_front, 2, 2, front)
+        close(early, whole)
+        fetch(vector_lookup, got_front, 2, 3, front)
+
+        got_back = neighbours("got_back", "wide", back)
+        for i in range(len(places)):
+            for tile in (2, 3):
+                fetch(scalar_lookup, got_back, i, tile, back)
+        bounds(got_front, late, front)
+        cap(got_front, late, front)
+        weave(nc.scalar.copy, o_bf[:, :, early], median[:, early, :])
+        bounds(got_back, late, back)
+        cap(got_back, late, back)
+        close(late, front)
+        weave(nc.scalar.copy, o_bf[:, front, late], median[:, late, front])
+        nc.vector.tensor_tensor(
+            by_runs_woven(o_bf[:, back, late]),
+            by_runs_apart(low[:, late, back]),
+            by_runs_apart(capped[:, late, back]),
+            MAX,
+        )
+        close(late, back)
+        hand_on(back)
+        hand_on(front)
 
         scale_rows = o_scales[:].bitcast(I32)
         for q in range(P // QUADRANT):

@@ -26,8 +26,6 @@ HALF_N = N // 2
 HALF_P = P // 2
 HALF_S = S // 2
 HALF_V = V // 2
-VECTOR_WEAVES = 384
-VECTOR_DEALS = 40
 
 
 def tile_picked_median_none_lo_kernel(
@@ -47,7 +45,7 @@ def tile_picked_median_none_lo_kernel(
         x_raw = [sb.tile([P, T], F32, name="x_raw%d" % j) for j in range(PACK)]
         w_first = sb.tile([P, HALF_N], F32, name="w_first")
         w_rest = sb.tile([P, PACK - 1, HALF_N], F32, name="w_rest")
-        w_last = sb.tile([P, PACK, HALF_N], F32, name="w_last")
+        w_last = sb.tile([P, PACK, HALF_N], F32, name="w_last", tag="last")
         picked = sb.tile([P, S // LIST], U16, name="picked")
         nc.sync.dma_start(out=w_first[:], in_=w_rows[:, 0, 0:HALF_N])
         nc.sync.dma_start(picked[:], offs)
@@ -72,8 +70,14 @@ def tile_picked_median_none_lo_kernel(
         codes = sb.tile([P, S + N], U32, name="codes", align_bytes=64)
         scales = sb.tile([P, S + N], U8, name="scales", align_bytes=64)
         x_bf = rounded[:, 0 : S * PACK].rearrange("p (s j) -> p s j", j=PACK)
-        w_bf = rounded[:, S * PACK :].rearrange("p (t m j) -> p t m j", t=PACK, j=PACK)
-        first_col = [S + tile * P for tile in range(PACK)]
+        first_col = [S, S + 3 * P, S + P, S + 2 * P]
+        mixed_bf = [
+            rounded[:, first_col[h] * PACK : (first_col[h] + P) * PACK].rearrange("p (t m j) -> p m j t", t=2, j=PACK)
+            for h in range(2)
+        ]
+        straight_bf = rounded[:, first_col[2] * PACK : (first_col[3] + P) * PACK].rearrange(
+            "p (t h m j) -> p h m j t", t=2, h=2, j=PACK
+        )
 
         def by_runs_woven(ap):
             return ap.rearrange("p (c i) e -> p c e i", i=RUN)
@@ -91,44 +95,32 @@ def tile_picked_median_none_lo_kernel(
                 in_=values[:, first * PACK : stop * PACK],
             )
 
-        def pick(lookup, j, cols):
-            lookup(x_picked[:, j, cols], x_raw[j][:].indirect(picked[:, cols.start // LIST : cols.stop // LIST]))
+        def by_tiles(w_raw):
+            return w_raw[:].rearrange("p j (m t) -> p m j t", t=PACK)
 
-        def weave_pair(engine_copy, j, cols):
-            weave(engine_copy, x_bf[:, cols, j : j + 2], x_picked[:, j : j + 2, cols])
-
-        def deal_last(engine_copy, ms, ts):
-            engine_copy(
-                out=w_bf[:, ts, HALF_P + ms.start : HALF_P + ms.stop, :].rearrange("p t m j -> p m j t"),
-                in_=w_last[:].rearrange("p j (m t) -> p m j t", t=PACK)[:, ms, :, ts],
-            )
-
-        nc.scalar.copy(
-            out=w_bf[:, :, 0:HALF_P, 0].rearrange("p t m -> p m t"),
-            in_=w_first[:].rearrange("p (m t) -> p m t", t=PACK),
-        )
+        first_by_tiles = w_first[:].rearrange("p (m t) -> p m t", t=PACK)
+        nc.scalar.copy(out=mixed_bf[0][:, :, 0, :], in_=first_by_tiles[:, :, 0:2])
+        nc.scalar.copy(out=straight_bf[:, 0, :, 0, :], in_=first_by_tiles[:, :, 2:4])
         for j in range(PACK):
-            pick(vector_lookup, j, slice(0, HALF_S))
-            pick(scalar_lookup, j, slice(HALF_S, S))
+            vector_lookup(x_picked[:, j, 0:HALF_S], x_raw[j][:].indirect(picked[:, 0 : HALF_S // LIST]))
+            scalar_lookup(x_picked[:, j, HALF_S:S], x_raw[j][:].indirect(picked[:, HALF_S // LIST : S // LIST]))
             if j % 2 == 1:
-                weave_pair(nc.vector.tensor_copy, j - 1, slice(0, HALF_S))
-                weave_pair(nc.vector.tensor_copy, j - 1, slice(HALF_S, VECTOR_WEAVES))
-                weave_pair(nc.scalar.copy, j - 1, slice(VECTOR_WEAVES, S))
+                for engine_copy, cols in (
+                    (nc.vector.tensor_copy, slice(0, HALF_S)),
+                    (nc.vector.tensor_copy, slice(HALF_S, S - P)),
+                    (nc.scalar.copy, slice(S - P, S)),
+                ):
+                    weave(engine_copy, x_bf[:, cols, j - 1 : j + 1], x_picked[:, j - 1 : j + 1, cols])
         quantize(codes, scales, rounded, 0, HALF_S)
+        nc.scalar.copy(out=mixed_bf[0][:, :, 1:PACK, :], in_=by_tiles(w_rest)[:, :, :, 0:2])
         quantize(codes, scales, rounded, HALF_S, S - P)
-        nc.scalar.copy(
-            out=w_bf[:, :, 0:HALF_P, 1:PACK].rearrange("p t m j -> p m j t"),
-            in_=w_rest[:].rearrange("p j (m t) -> p m j t", t=PACK),
-        )
-        early, late = slice(0, 2), slice(2, PACK)
-        deal_last(nc.vector.tensor_copy, slice(0, VECTOR_DEALS), early)
-        deal_last(nc.scalar.copy, slice(VECTOR_DEALS, HALF_P), early)
-        quantize(codes, scales, rounded, first_col[1], first_col[1] + P)
         quantize(codes, scales, rounded, S - P, first_col[0] + P)
-        deal_last(nc.scalar.copy, slice(0, HALF_P), late)
-        quantize(codes, scales, rounded, first_col[2], first_col[3] + P)
+        nc.scalar.copy(out=straight_bf[:, 0, :, 1:PACK, :], in_=by_tiles(w_rest)[:, :, :, 2:4])
+        nc.vector.tensor_copy(out=mixed_bf[1], in_=by_tiles(w_last)[:, :, :, 0:2])
+        nc.scalar.copy(out=straight_bf[:, 1], in_=by_tiles(w_last)[:, :, :, 2:4])
+        quantize(codes, scales, rounded, first_col[1], first_col[1] + P)
 
-        y = [sb.tile([P, S], F32, name="y%d" % tile, tag="y%d" % (tile % 3)) for tile in range(PACK)]
+        y = [sb.tile([P, S], F32, name="y%d" % tile, tag=("last", "y1", "y2", "y3")[tile]) for tile in range(PACK)]
 
         def product(bank, tile, cols):
             acc = ps.tile([P, cols.stop - cols.start], F32, name=bank)
@@ -145,27 +137,35 @@ def tile_picked_median_none_lo_kernel(
             return acc
 
         pieces = (slice(0, HALF_S), slice(HALF_S, S - P), slice(S - P, S))
-        first_banks = [product("acc1%d" % b, 1, pieces[b]) for b in range(len(pieces))]
-        banks = {tile: product("acc%d" % tile, tile, slice(0, S)) for tile in (0, 2, 3)}
+        first_banks = [product("acc0%d" % b, 0, pieces[b]) for b in range(len(pieces))]
+        banks = {1: product("acc1", 1, slice(0, S))}
+        for b, engine_copy in enumerate((nc.vector.tensor_copy, nc.scalar.copy, nc.scalar.copy)):
+            engine_copy(out=y[0][:, pieces[b]], in_=first_banks[b][:])
+        quantize(codes, scales, rounded, first_col[2], first_col[3] + P)
+        for tile in (2, 3):
+            banks[tile] = product("acc%d" % tile, tile, slice(0, S))
 
         high = sb.tile([P, PACK, V], F32, name="high")
         low = sb.tile([P, PACK, V], F32, name="low")
         capped = sb.tile([P, PACK, V], F32, name="capped")
-        median = sb.tile([P, PACK, V], F32, name="median")
+        mixed = [sb.tile([P, V], F32, name="mixed%d" % h) for h in range(2)]
+        regrouped = sb.tile([P, 2, V], F32, name="regrouped")
+        median = sb.tile([P, 2, V], F32, name="median")
         o_bf = sb.tile([P, V, PACK], BF16, name="o_bf", align_bytes=64)
         o_codes = sb.tile([P, V], U32, name="o_codes", align_bytes=64)
         o_scales = sb.tile([P, V], U8, name="o_scales", align_bytes=64)
         o_flat = o_bf[:].rearrange("p v t -> p (v t)")
         whole, front, back = slice(0, V), slice(0, HALF_V), slice(HALF_V, V)
+        early, late = slice(0, 2), slice(2, PACK)
 
-        def neighbours(name, tag, vs):
+        def neighbours(name, tag, tiles, vs):
             return [
-                sb.tile([P, 2, vs.stop - vs.start], F32, name="%s%d" % (name, i), tag="%s%d" % (tag, i))
+                sb.tile([P, tiles, vs.stop - vs.start], F32, name="%s%d" % (name, i), tag="%s%d" % (tag, i))
                 for i in range(len(places))
             ]
 
-        def fetch(lookup, got, i, tile, vs):
-            lookup(got[i][:, tile % 2, :], y[tile][:].indirect(places[i][:, vs.start // LIST : vs.stop // LIST]))
+        def fetch(lookup, dst, i, tile, vs):
+            lookup(dst, y[tile][:].indirect(places[i][:, vs.start // LIST : vs.stop // LIST]))
 
         def bounds(got, ts, vs):
             nc.vector.tensor_tensor(high[:, ts, vs], got[0][:], got[1][:], MAX)
@@ -174,55 +174,67 @@ def tile_picked_median_none_lo_kernel(
         def cap(got, ts, vs):
             nc.vector.tensor_tensor(capped[:, ts, vs], high[:, ts, vs], got[2][:], MIN)
 
-        def close(ts, vs):
-            nc.vector.tensor_tensor(median[:, ts, vs], low[:, ts, vs], capped[:, ts, vs], MAX)
-            nc.sync.dma_start(out=out_rows[:, ts, vs], in_=median[:, ts, vs])
+        def close_mixed(h):
+            nc.vector.tensor_tensor(mixed[h][:], low[:, h, :], capped[:, h, :], MAX)
+            home = slice(h * HALF_P, (h + 1) * HALF_P)
+            for t in range(2):
+                nc.sync.dma_start(out=regrouped[home, t, :], in_=mixed[h][t * HALF_P : (t + 1) * HALF_P, :])
+            for t in range(2):
+                nc.sync.dma_start(out=out_rows[home, t, :], in_=mixed[h][t * HALF_P : (t + 1) * HALF_P, :])
+
+        def close(vs):
+            nc.vector.tensor_tensor(median[:, :, vs], low[:, late, vs], capped[:, late, vs], MAX)
+            nc.sync.dma_start(out=out_rows[:, late, vs], in_=median[:, :, vs])
 
         def hand_on(vs):
             quantize(o_codes, o_scales, o_flat, vs.start, vs.stop)
             nc.scalar.dma_start(out=out_words[:, vs], in_=o_codes[:, vs].bitcast(I32))
 
-        for b, engine_copy in enumerate((nc.vector.tensor_copy, nc.scalar.copy, nc.scalar.copy)):
-            engine_copy(out=y[1][:, pieces[b]], in_=first_banks[b][:])
-        got_early = neighbours("got_early", "wide", whole)
+        def slot(name, tag, tiles, vs):
+            return sb.tile([P, tiles, vs.stop - vs.start], F32, name=name, tag=tag)
+
+        got0 = [slot("got0_%d" % i, "first%d" % i, 1, whole) for i in range(3)]
+        got1 = [slot("got1_0", "second0", 1, whole), slot("got1_1", "second1", 1, whole), slot("got1_2", "first0", 1, whole)]
+        got_front = [slot("front0", "front0", 2, front), slot("front1", "front1", 2, front), slot("front2", "second1", 2, front)]
+        got_back = neighbours("got_back", "back", 2, back)
         for i in range(2):
-            fetch(scalar_lookup, got_early, i, 1, whole)
-        nc.vector.tensor_copy(out=y[0][:], in_=banks[0][:])
-        fetch(vector_lookup, got_early, 2, 1, whole)
-        for i in range(2):
-            fetch(scalar_lookup, got_early, i, 0, whole)
-        fetch(vector_lookup, got_early, 2, 0, whole)
+            fetch(scalar_lookup, got0[i][:, 0, :], i, 0, whole)
+        fetch(vector_lookup, got0[2][:, 0, :], 2, 0, whole)
+        nc.vector.tensor_copy(out=y[1][:], in_=banks[1][:])
         nc.vector.tensor_copy(out=y[2][:], in_=banks[2][:])
+        for i in range(2):
+            fetch(scalar_lookup, got1[i][:, 0, :], i, 1, whole)
         nc.scalar.copy(out=y[3][:], in_=banks[3][:])
-
-        got_front = neighbours("got_front", "narrow", front)
+        bounds(got0, slice(0, 1), whole)
+        cap(got0, slice(0, 1), whole)
+        fetch(vector_lookup, got1[2][:, 0, :], 2, 1, whole)
+        close_mixed(0)
+        bounds(got1, slice(1, 2), whole)
+        cap(got1, slice(1, 2), whole)
+        fetch(vector_lookup, got_front[2][:, 0, :], 2, 2, front)
+        close_mixed(1)
+        fetch(vector_lookup, got_front[2][:, 1, :], 2, 3, front)
         for i in range(2):
             for tile in (2, 3):
-                fetch(scalar_lookup, got_front, i, tile, front)
-        bounds(got_early, early, whole)
-        cap(got_early, early, whole)
-        fetch(vector_lookup, got_front, 2, 2, front)
-        close(early, whole)
-        fetch(vector_lookup, got_front, 2, 3, front)
-
-        got_back = neighbours("got_back", "wide", back)
-        for i in range(len(places)):
+                fetch(scalar_lookup, got_front[i][:, tile - 2, :], i, tile, front)
+        for i in range(3):
             for tile in (2, 3):
-                fetch(scalar_lookup, got_back, i, tile, back)
+                fetch(scalar_lookup, got_back[i][:, tile - 2, :], i, tile, back)
         bounds(got_front, late, front)
         cap(got_front, late, front)
-        weave(nc.scalar.copy, o_bf[:, :, early], median[:, early, :])
         bounds(got_back, late, back)
+        close(front)
         cap(got_back, late, back)
-        close(late, front)
-        weave(nc.scalar.copy, o_bf[:, front, late], median[:, late, front])
+        weave(nc.scalar.copy, o_bf[:, back, early], regrouped[:, :, back])
+        weave(nc.scalar.copy, o_bf[:, front, early], regrouped[:, :, front])
+        weave(nc.scalar.copy, o_bf[:, front, late], median[:, :, front])
         nc.vector.tensor_tensor(
             by_runs_woven(o_bf[:, back, late]),
             by_runs_apart(low[:, late, back]),
             by_runs_apart(capped[:, late, back]),
             MAX,
         )
-        close(late, back)
+        close(back)
         hand_on(back)
         hand_on(front)
 

@@ -18,6 +18,7 @@ COPY = mybir.ActivationFunctionType.Copy
 
 P = 128
 PACK = 4
+PAIR = 2
 LIST = 16
 RUN = 4
 QUADRANT = 32
@@ -41,13 +42,16 @@ def tile_picked_median_none_lo_kernel(
         out_rows = out_0.rearrange("(p t) v -> p t v", t=PACK)
         out_words = out_1[0].rearrange("p c r -> p (c r)").bitcast(I32)
         out_scales = out_2[0].bitcast(I32)
+        low_pair, high_pair = slice(0, PAIR), slice(PAIR, PACK)
+        first_half, second_half = slice(0, HALF_S), slice(HALF_S, S)
+        third_quarter, last_quarter = slice(HALF_S, S - P), slice(S - P, S)
 
         x_raw = [sb.tile([P, T], F32, name="x_raw%d" % j) for j in range(PACK)]
-        w_first = sb.tile([P, HALF_N], F32, name="w_first")
+        w_first = sb.tile([P, 1, HALF_N], F32, name="w_first")
         w_rest = sb.tile([P, PACK - 1, HALF_N], F32, name="w_rest")
-        w_last = sb.tile([P, PACK, HALF_N], F32, name="w_last", tag="last")
+        w_last = sb.tile([P, PACK, HALF_N], F32, name="w_last", tag="w_last")
         picked = sb.tile([P, S // LIST], U16, name="picked")
-        nc.sync.dma_start(out=w_first[:], in_=w_rows[:, 0, 0:HALF_N])
+        nc.sync.dma_start(out=w_first[:], in_=w_rows[:, 0:1, 0:HALF_N])
         nc.sync.dma_start(picked[:], offs)
         for j in range(PACK):
             nc.sync.dma_start(out=x_raw[j][:], in_=x_rows[:, j, :])
@@ -65,19 +69,8 @@ def tile_picked_median_none_lo_kernel(
         def scalar_lookup(dst, src):
             nc.scalar.activation(dst, src, COPY)
 
-        x_picked = sb.tile([P, PACK, S], BF16, name="x_picked")
-        rounded = sb.tile([P, (S + N) * PACK], BF16, name="rounded", align_bytes=64)
-        codes = sb.tile([P, S + N], U32, name="codes", align_bytes=64)
-        scales = sb.tile([P, S + N], U8, name="scales", align_bytes=64)
-        x_bf = rounded[:, 0 : S * PACK].rearrange("p (s j) -> p s j", j=PACK)
-        first_col = [S, S + 3 * P, S + P, S + 2 * P]
-        mixed_bf = [
-            rounded[:, first_col[h] * PACK : (first_col[h] + P) * PACK].rearrange("p (t m j) -> p m j t", t=2, j=PACK)
-            for h in range(2)
-        ]
-        straight_bf = rounded[:, first_col[2] * PACK : (first_col[3] + P) * PACK].rearrange(
-            "p (t h m j) -> p h m j t", t=2, h=2, j=PACK
-        )
+        def entries(list_tile, span):
+            return list_tile[:, span.start // LIST : span.stop // LIST]
 
         def by_runs_woven(ap):
             return ap.rearrange("p (c i) e -> p c e i", i=RUN)
@@ -88,47 +81,71 @@ def tile_picked_median_none_lo_kernel(
         def weave(engine_copy, dst, src):
             engine_copy(out=by_runs_woven(dst), in_=by_runs_apart(src))
 
-        def quantize(words, scale_bytes, values, first, stop):
-            nc.vector.quantize_mx(
-                out=words[:, first:stop].bitcast(FP8X4),
-                scales=scale_bytes[:, first:stop],
-                in_=values[:, first * PACK : stop * PACK],
+        def quantize(words, scale_bytes, values):
+            nc.vector.quantize_mx(out=words.bitcast(FP8X4), scales=scale_bytes, in_=values)
+
+        x_picked = sb.tile([P, PACK, S], BF16, name="x_picked")
+        rounded = sb.tile([P, (S + N) * PACK], BF16, name="rounded", align_bytes=64)
+        codes = sb.tile([P, S + N], U32, name="codes", align_bytes=64)
+        scales = sb.tile([P, S + N], U8, name="scales", align_bytes=64)
+        w_cols = [slice(S + slot * P, S + (slot + 1) * P) for slot in (0, 3, 1, 2)]
+        straight_cols = slice(w_cols[2].start, w_cols[3].stop)
+
+        def values_of(flat, cols):
+            return flat[:, cols.start * PACK : cols.stop * PACK]
+
+        def quantize_operands(cols):
+            quantize(codes[:, cols], scales[:, cols], values_of(rounded, cols))
+
+        x_woven = values_of(rounded, slice(0, S)).rearrange("p (s j) -> p s j", j=PACK)
+        mixed_dealt = [
+            values_of(rounded, w_cols[h]).rearrange("p (t m j) -> p m j t", t=PAIR, j=PACK) for h in range(PAIR)
+        ]
+        straight_dealt = values_of(rounded, straight_cols).rearrange("p (t h m j) -> p h m j t", t=PAIR, h=PAIR, j=PACK)
+
+        def deal_mixed(engine_copy, h, js, w_raw):
+            engine_copy(
+                out=mixed_dealt[h][:, :, js, :],
+                in_=w_raw[:].rearrange("p j (m t) -> p m j t", t=PACK)[:, :, :, low_pair],
             )
 
-        def by_tiles(w_raw):
-            return w_raw[:].rearrange("p j (m t) -> p m j t", t=PACK)
+        def deal_straight(engine_copy, h, js, w_raw):
+            engine_copy(
+                out=straight_dealt[:, h, :, js, :],
+                in_=w_raw[:].rearrange("p j (m t) -> p m j t", t=PACK)[:, :, :, high_pair],
+            )
 
-        first_by_tiles = w_first[:].rearrange("p (m t) -> p m t", t=PACK)
-        nc.scalar.copy(out=mixed_bf[0][:, :, 0, :], in_=first_by_tiles[:, :, 0:2])
-        nc.scalar.copy(out=straight_bf[:, 0, :, 0, :], in_=first_by_tiles[:, :, 2:4])
+        def weave_picked(engine_copy, js, cols):
+            weave(engine_copy, x_woven[:, cols, js], x_picked[:, js, cols])
+
+        deal_mixed(nc.scalar.copy, 0, slice(0, 1), w_first)
+        deal_straight(nc.scalar.copy, 0, slice(0, 1), w_first)
         for j in range(PACK):
-            vector_lookup(x_picked[:, j, 0:HALF_S], x_raw[j][:].indirect(picked[:, 0 : HALF_S // LIST]))
-            scalar_lookup(x_picked[:, j, HALF_S:S], x_raw[j][:].indirect(picked[:, HALF_S // LIST : S // LIST]))
-            if j % 2 == 1:
-                for engine_copy, cols in (
-                    (nc.vector.tensor_copy, slice(0, HALF_S)),
-                    (nc.vector.tensor_copy, slice(HALF_S, S - P)),
-                    (nc.scalar.copy, slice(S - P, S)),
-                ):
-                    weave(engine_copy, x_bf[:, cols, j - 1 : j + 1], x_picked[:, j - 1 : j + 1, cols])
-        quantize(codes, scales, rounded, 0, HALF_S)
-        nc.scalar.copy(out=mixed_bf[0][:, :, 1:PACK, :], in_=by_tiles(w_rest)[:, :, :, 0:2])
-        quantize(codes, scales, rounded, HALF_S, S - P)
-        quantize(codes, scales, rounded, S - P, first_col[0] + P)
-        nc.scalar.copy(out=straight_bf[:, 0, :, 1:PACK, :], in_=by_tiles(w_rest)[:, :, :, 2:4])
-        nc.vector.tensor_copy(out=mixed_bf[1], in_=by_tiles(w_last)[:, :, :, 0:2])
-        nc.scalar.copy(out=straight_bf[:, 1], in_=by_tiles(w_last)[:, :, :, 2:4])
-        quantize(codes, scales, rounded, first_col[1], first_col[1] + P)
+            vector_lookup(x_picked[:, j, first_half], x_raw[j][:].indirect(entries(picked, first_half)))
+            scalar_lookup(x_picked[:, j, second_half], x_raw[j][:].indirect(entries(picked, second_half)))
+            if j % PAIR == PAIR - 1:
+                js = slice(j + 1 - PAIR, j + 1)
+                weave_picked(nc.vector.tensor_copy, js, first_half)
+                weave_picked(nc.vector.tensor_copy, js, third_quarter)
+                weave_picked(nc.scalar.copy, js, last_quarter)
+        quantize_operands(first_half)
+        deal_mixed(nc.scalar.copy, 0, slice(1, PACK), w_rest)
+        quantize_operands(third_quarter)
+        quantize_operands(slice(last_quarter.start, w_cols[0].stop))
+        deal_straight(nc.scalar.copy, 0, slice(1, PACK), w_rest)
+        deal_mixed(nc.vector.tensor_copy, 1, slice(0, PACK), w_last)
+        deal_straight(nc.scalar.copy, 1, slice(0, PACK), w_last)
+        quantize_operands(w_cols[1])
 
-        y = [sb.tile([P, S], F32, name="y%d" % tile, tag=("last", "y1", "y2", "y3")[tile]) for tile in range(PACK)]
+        y = [sb.tile([P, S], F32, name="y0", tag="w_last")]
+        y.extend(sb.tile([P, S], F32, name="y%d" % tile) for tile in range(1, PACK))
 
-        def product(bank, tile, cols):
-            acc = ps.tile([P, cols.stop - cols.start], F32, name=bank)
-            w_cols = slice(first_col[tile], first_col[tile] + P)
+        def product(tile, cols):
+            acc = ps.tile([P, cols.stop - cols.start], F32, name="acc%d_%d" % (tile, cols.start))
             nc.tensor.matmul_mx(
                 out=acc[:],
-                lhsT=codes[:, w_cols].bitcast(FP8X4),
-                lhsT_scale=scales[:, w_cols],
+                lhsT=codes[:, w_cols[tile]].bitcast(FP8X4),
+                lhsT_scale=scales[:, w_cols[tile]],
                 rhs=codes[:, cols].bitcast(FP8X4),
                 rhs_scale=scales[:, cols],
                 start=True,
@@ -136,107 +153,96 @@ def tile_picked_median_none_lo_kernel(
             )
             return acc
 
-        pieces = (slice(0, HALF_S), slice(HALF_S, S - P), slice(S - P, S))
-        first_banks = [product("acc0%d" % b, 0, pieces[b]) for b in range(len(pieces))]
-        banks = {1: product("acc1", 1, slice(0, S))}
-        for b, engine_copy in enumerate((nc.vector.tensor_copy, nc.scalar.copy, nc.scalar.copy)):
-            engine_copy(out=y[0][:, pieces[b]], in_=first_banks[b][:])
-        quantize(codes, scales, rounded, first_col[2], first_col[3] + P)
-        for tile in (2, 3):
-            banks[tile] = product("acc%d" % tile, tile, slice(0, S))
+        pieces = (first_half, third_quarter, last_quarter)
+        first_banks = [product(0, cols) for cols in pieces]
+        banks = {1: product(1, slice(0, S))}
+        for bank, cols, engine_copy in zip(first_banks, pieces, (nc.vector.tensor_copy, nc.scalar.copy, nc.scalar.copy)):
+            engine_copy(out=y[0][:, cols], in_=bank[:])
+        quantize_operands(straight_cols)
+        for tile in range(PAIR, PACK):
+            banks[tile] = product(tile, slice(0, S))
 
         high = sb.tile([P, PACK, V], F32, name="high")
         low = sb.tile([P, PACK, V], F32, name="low")
         capped = sb.tile([P, PACK, V], F32, name="capped")
-        mixed = [sb.tile([P, V], F32, name="mixed%d" % h) for h in range(2)]
-        regrouped = sb.tile([P, 2, V], F32, name="regrouped")
-        median = sb.tile([P, 2, V], F32, name="median")
+        mixed = [sb.tile([P, V], F32, name="mixed%d" % h) for h in range(PAIR)]
+        regrouped = sb.tile([P, PAIR, V], F32, name="regrouped")
+        straight = sb.tile([P, PAIR, V], F32, name="straight")
         o_bf = sb.tile([P, V, PACK], BF16, name="o_bf", align_bytes=64)
         o_codes = sb.tile([P, V], U32, name="o_codes", align_bytes=64)
         o_scales = sb.tile([P, V], U8, name="o_scales", align_bytes=64)
         o_flat = o_bf[:].rearrange("p v t -> p (v t)")
         whole, front, back = slice(0, V), slice(0, HALF_V), slice(HALF_V, V)
-        early, late = slice(0, 2), slice(2, PACK)
 
-        def neighbours(name, tag, tiles, vs):
-            return [
-                sb.tile([P, tiles, vs.stop - vs.start], F32, name="%s%d" % (name, i), tag="%s%d" % (tag, i))
-                for i in range(len(places))
-            ]
+        def neighbours(name, tiles, vs, buffers):
+            shape = [P, tiles.stop - tiles.start, vs.stop - vs.start]
+            return [sb.tile(shape, F32, name="%s%d" % (name, i), tag=buffers[i]) for i in range(len(places))]
 
-        def fetch(lookup, dst, i, tile, vs):
-            lookup(dst, y[tile][:].indirect(places[i][:, vs.start // LIST : vs.stop // LIST]))
+        def fetch(lookup, got, i, slot, tile, vs):
+            lookup(got[i][:, slot, :], y[tile][:].indirect(entries(places[i], vs)))
 
-        def bounds(got, ts, vs):
-            nc.vector.tensor_tensor(high[:, ts, vs], got[0][:], got[1][:], MAX)
-            nc.vector.tensor_tensor(low[:, ts, vs], got[0][:], got[1][:], MIN)
+        def bounds(got, tiles, vs):
+            nc.vector.tensor_tensor(high[:, tiles, vs], got[0][:], got[1][:], MAX)
+            nc.vector.tensor_tensor(low[:, tiles, vs], got[0][:], got[1][:], MIN)
 
-        def cap(got, ts, vs):
-            nc.vector.tensor_tensor(capped[:, ts, vs], high[:, ts, vs], got[2][:], MIN)
+        def cap(got, tiles, vs):
+            nc.vector.tensor_tensor(capped[:, tiles, vs], high[:, tiles, vs], got[2][:], MIN)
 
         def close_mixed(h):
             nc.vector.tensor_tensor(mixed[h][:], low[:, h, :], capped[:, h, :], MAX)
-            home = slice(h * HALF_P, (h + 1) * HALF_P)
-            for t in range(2):
-                nc.sync.dma_start(out=regrouped[home, t, :], in_=mixed[h][t * HALF_P : (t + 1) * HALF_P, :])
-            for t in range(2):
-                nc.sync.dma_start(out=out_rows[home, t, :], in_=mixed[h][t * HALF_P : (t + 1) * HALF_P, :])
+            for rows in (regrouped, out_rows):
+                for t in range(PAIR):
+                    nc.sync.dma_start(
+                        out=rows[h * HALF_P : (h + 1) * HALF_P, t, :], in_=mixed[h][t * HALF_P : (t + 1) * HALF_P, :]
+                    )
 
-        def close(vs):
-            nc.vector.tensor_tensor(median[:, :, vs], low[:, late, vs], capped[:, late, vs], MAX)
-            nc.sync.dma_start(out=out_rows[:, late, vs], in_=median[:, :, vs])
+        def close_straight(vs):
+            nc.vector.tensor_tensor(straight[:, :, vs], low[:, high_pair, vs], capped[:, high_pair, vs], MAX)
+            nc.sync.dma_start(out=out_rows[:, high_pair, vs], in_=straight[:, :, vs])
 
-        def hand_on(vs):
-            quantize(o_codes, o_scales, o_flat, vs.start, vs.stop)
-            nc.scalar.dma_start(out=out_words[:, vs], in_=o_codes[:, vs].bitcast(I32))
-
-        def slot(name, tag, tiles, vs):
-            return sb.tile([P, tiles, vs.stop - vs.start], F32, name=name, tag=tag)
-
-        got0 = [slot("got0_%d" % i, "first%d" % i, 1, whole) for i in range(3)]
-        got1 = [slot("got1_0", "second0", 1, whole), slot("got1_1", "second1", 1, whole), slot("got1_2", "first0", 1, whole)]
-        got_front = [slot("front0", "front0", 2, front), slot("front1", "front1", 2, front), slot("front2", "second1", 2, front)]
-        got_back = neighbours("got_back", "back", 2, back)
+        tile0, tile1 = slice(0, 1), slice(1, PAIR)
+        got0 = neighbours("got0_", tile0, whole, ("a0", "a1", "a2"))
+        got1 = neighbours("got1_", tile1, whole, ("b0", "b1", "a0"))
+        got_front = neighbours("got_front", high_pair, front, ("c0", "c1", "b1"))
+        got_back = neighbours("got_back", high_pair, back, ("d0", "d1", "d2"))
         for i in range(2):
-            fetch(scalar_lookup, got0[i][:, 0, :], i, 0, whole)
-        fetch(vector_lookup, got0[2][:, 0, :], 2, 0, whole)
-        nc.vector.tensor_copy(out=y[1][:], in_=banks[1][:])
-        nc.vector.tensor_copy(out=y[2][:], in_=banks[2][:])
+            fetch(scalar_lookup, got0, i, 0, 0, whole)
+        fetch(vector_lookup, got0, 2, 0, 0, whole)
+        for tile in (1, 2):
+            nc.vector.tensor_copy(out=y[tile][:], in_=banks[tile][:])
         for i in range(2):
-            fetch(scalar_lookup, got1[i][:, 0, :], i, 1, whole)
+            fetch(scalar_lookup, got1, i, 0, 1, whole)
         nc.scalar.copy(out=y[3][:], in_=banks[3][:])
-        bounds(got0, slice(0, 1), whole)
-        cap(got0, slice(0, 1), whole)
-        fetch(vector_lookup, got1[2][:, 0, :], 2, 1, whole)
+        bounds(got0, tile0, whole)
+        cap(got0, tile0, whole)
+        fetch(vector_lookup, got1, 2, 0, 1, whole)
         close_mixed(0)
-        bounds(got1, slice(1, 2), whole)
-        cap(got1, slice(1, 2), whole)
-        fetch(vector_lookup, got_front[2][:, 0, :], 2, 2, front)
+        bounds(got1, tile1, whole)
+        cap(got1, tile1, whole)
+        fetch(vector_lookup, got_front, 2, 0, 2, front)
         close_mixed(1)
-        fetch(vector_lookup, got_front[2][:, 1, :], 2, 3, front)
-        for i in range(2):
-            for tile in (2, 3):
-                fetch(scalar_lookup, got_front[i][:, tile - 2, :], i, tile, front)
-        for i in range(3):
-            for tile in (2, 3):
-                fetch(scalar_lookup, got_back[i][:, tile - 2, :], i, tile, back)
-        bounds(got_front, late, front)
-        cap(got_front, late, front)
-        bounds(got_back, late, back)
-        close(front)
-        cap(got_back, late, back)
-        weave(nc.scalar.copy, o_bf[:, back, early], regrouped[:, :, back])
-        weave(nc.scalar.copy, o_bf[:, front, early], regrouped[:, :, front])
-        weave(nc.scalar.copy, o_bf[:, front, late], median[:, :, front])
+        fetch(vector_lookup, got_front, 2, 1, 3, front)
+        for got, vs, count in ((got_front, front, 2), (got_back, back, 3)):
+            for i in range(count):
+                for slot in range(PAIR):
+                    fetch(scalar_lookup, got, i, slot, PAIR + slot, vs)
+        for got, vs in ((got_front, front), (got_back, back)):
+            bounds(got, high_pair, vs)
+            cap(got, high_pair, vs)
+        close_straight(front)
+        weave(nc.scalar.copy, o_bf[:, front, high_pair], straight[:, :, front])
+        weave(nc.scalar.copy, o_bf[:, front, low_pair], regrouped[:, :, front])
         nc.vector.tensor_tensor(
-            by_runs_woven(o_bf[:, back, late]),
-            by_runs_apart(low[:, late, back]),
-            by_runs_apart(capped[:, late, back]),
+            by_runs_woven(o_bf[:, back, high_pair]),
+            by_runs_apart(low[:, high_pair, back]),
+            by_runs_apart(capped[:, high_pair, back]),
             MAX,
         )
-        close(back)
-        hand_on(back)
-        hand_on(front)
+        close_straight(back)
+        weave(nc.vector.tensor_copy, o_bf[:, back, low_pair], regrouped[:, :, back])
+        for vs in (back, front):
+            quantize(o_codes[:, vs], o_scales[:, vs], values_of(o_flat, vs))
+        nc.sync.dma_start(out=out_words, in_=o_codes[:].bitcast(I32))
 
         scale_rows = o_scales[:].bitcast(I32)
         for q in range(P // QUADRANT):

@@ -23,6 +23,7 @@ LIST = 16
 RUN = 4
 QUADRANT = 32
 SCALE_ROWS = 4
+LONG_ROW = 256
 HALF_N = N // 2
 HALF_P = P // 2
 HALF_S = S // 2
@@ -44,12 +45,11 @@ def tile_picked_median_none_lo_kernel(
         out_scales = out_2[0].bitcast(I32)
         low_pair, high_pair = slice(0, PAIR), slice(PAIR, PACK)
         first_half, second_half = slice(0, HALF_S), slice(HALF_S, S)
-        third_quarter, last_quarter = slice(HALF_S, S - P), slice(S - P, S)
 
-        x_raw = [sb.tile([P, T], F32, name="x_raw%d" % j) for j in range(PACK)]
-        w_first = sb.tile([P, 1, HALF_N], F32, name="w_first")
-        w_rest = sb.tile([P, PACK - 1, HALF_N], F32, name="w_rest")
-        w_last = sb.tile([P, PACK, HALF_N], F32, name="w_last", tag="w_last")
+        x_raw = [sb.tile([P, T], F32, name="x_raw%d" % j, align_bytes=LONG_ROW) for j in range(PACK)]
+        w_first = sb.tile([P, 1, HALF_N], F32, name="w_first", align_bytes=LONG_ROW)
+        w_rest = sb.tile([P, PACK - 1, HALF_N], F32, name="w_rest", align_bytes=LONG_ROW)
+        w_last = sb.tile([P, PACK, HALF_N], F32, name="w_last", tag="w_last", align_bytes=LONG_ROW)
         picked = sb.tile([P, S // LIST], U16, name="picked")
         nc.sync.dma_start(out=w_first[:], in_=w_rows[:, 0:1, 0:HALF_N])
         nc.sync.dma_start(picked[:], offs)
@@ -84,11 +84,11 @@ def tile_picked_median_none_lo_kernel(
         def quantize(words, scale_bytes, values):
             nc.vector.quantize_mx(out=words.bitcast(FP8X4), scales=scale_bytes, in_=values)
 
-        x_picked = sb.tile([P, PACK, S], BF16, name="x_picked")
+        x_picked = sb.tile([P, PACK, HALF_S], BF16, name="x_picked")
         rounded = sb.tile([P, (S + N) * PACK], BF16, name="rounded", align_bytes=64)
         codes = sb.tile([P, S + N], U32, name="codes", align_bytes=64)
         scales = sb.tile([P, S + N], U8, name="scales", align_bytes=64)
-        w_cols = [slice(S + slot * P, S + (slot + 1) * P) for slot in (0, 3, 1, 2)]
+        w_cols = [slice(S + tile * P, S + (tile + 1) * P) for tile in range(PACK)]
         straight_cols = slice(w_cols[2].start, w_cols[3].stop)
 
         def values_of(flat, cols):
@@ -115,29 +115,24 @@ def tile_picked_median_none_lo_kernel(
                 in_=w_raw[:].rearrange("p j (m t) -> p m j t", t=PACK)[:, :, :, high_pair],
             )
 
-        def weave_picked(engine_copy, js, cols):
-            weave(engine_copy, x_woven[:, cols, js], x_picked[:, js, cols])
-
         deal_mixed(nc.scalar.copy, 0, slice(0, 1), w_first)
         deal_straight(nc.scalar.copy, 0, slice(0, 1), w_first)
         for j in range(PACK):
-            vector_lookup(x_picked[:, j, first_half], x_raw[j][:].indirect(entries(picked, first_half)))
-            scalar_lookup(x_picked[:, j, second_half], x_raw[j][:].indirect(entries(picked, second_half)))
+            vector_lookup(x_picked[:, j, :], x_raw[j][:].indirect(entries(picked, second_half)))
+            scalar_lookup(x_woven[:, first_half, j], x_raw[j][:].indirect(entries(picked, first_half)))
             if j % PAIR == PAIR - 1:
                 js = slice(j + 1 - PAIR, j + 1)
-                weave_picked(nc.vector.tensor_copy, js, first_half)
-                weave_picked(nc.vector.tensor_copy, js, third_quarter)
-                weave_picked(nc.scalar.copy, js, last_quarter)
+                weave(nc.vector.tensor_copy, x_woven[:, second_half, js], x_picked[:, js, :])
         quantize_operands(first_half)
         deal_mixed(nc.scalar.copy, 0, slice(1, PACK), w_rest)
-        quantize_operands(third_quarter)
-        quantize_operands(slice(last_quarter.start, w_cols[0].stop))
+        quantize_operands(w_cols[0])
+        quantize_operands(second_half)
         deal_straight(nc.scalar.copy, 0, slice(1, PACK), w_rest)
         deal_mixed(nc.vector.tensor_copy, 1, slice(0, PACK), w_last)
         deal_straight(nc.scalar.copy, 1, slice(0, PACK), w_last)
         quantize_operands(w_cols[1])
 
-        y = [sb.tile([P, S], F32, name="y0", tag="w_last")]
+        y = [sb.tile([P, S], F32, name="y0", tag="w_last", align_bytes=LONG_ROW)]
         y.extend(sb.tile([P, S], F32, name="y%d" % tile) for tile in range(1, PACK))
 
         def product(tile, cols):
@@ -153,10 +148,10 @@ def tile_picked_median_none_lo_kernel(
             )
             return acc
 
-        pieces = (first_half, third_quarter, last_quarter)
-        first_banks = [product(0, cols) for cols in pieces]
+        halves = (first_half, second_half)
+        first_banks = [product(0, cols) for cols in halves]
         banks = {1: product(1, slice(0, S))}
-        for bank, cols, engine_copy in zip(first_banks, pieces, (nc.vector.tensor_copy, nc.scalar.copy, nc.scalar.copy)):
+        for bank, cols, engine_copy in zip(first_banks, halves, (nc.scalar.copy, nc.vector.tensor_copy)):
             engine_copy(out=y[0][:, cols], in_=bank[:])
         quantize_operands(straight_cols)
         for tile in range(PAIR, PACK):
@@ -166,81 +161,66 @@ def tile_picked_median_none_lo_kernel(
         low = sb.tile([P, PACK, V], F32, name="low")
         capped = sb.tile([P, PACK, V], F32, name="capped")
         mixed = [sb.tile([P, V], F32, name="mixed%d" % h) for h in range(PAIR)]
-        regrouped = sb.tile([P, PAIR, V], F32, name="regrouped")
-        straight = sb.tile([P, PAIR, V], F32, name="straight")
+        medians = sb.tile([P, PACK, V], F32, name="medians")
         o_bf = sb.tile([P, V, PACK], BF16, name="o_bf", align_bytes=64)
         o_codes = sb.tile([P, V], U32, name="o_codes", align_bytes=64)
         o_scales = sb.tile([P, V], U8, name="o_scales", align_bytes=64)
         o_flat = o_bf[:].rearrange("p v t -> p (v t)")
         whole, front, back = slice(0, V), slice(0, HALF_V), slice(HALF_V, V)
 
-        def neighbours(name, tiles, vs, buffers):
-            shape = [P, tiles.stop - tiles.start, vs.stop - vs.start]
-            return [sb.tile(shape, F32, name="%s%d" % (name, i), tag=buffers[i]) for i in range(len(places))]
+        def fetch(lookup, i, tile, buffer):
+            got = sb.tile([P, V], F32, name="got%d_%d" % (tile, i), tag=buffer)
+            lookup(got[:], y[tile][:].indirect(places[i][:]))
+            return got
 
-        def fetch(lookup, got, i, slot, tile, vs):
-            lookup(got[i][:, slot, :], y[tile][:].indirect(entries(places[i], vs)))
+        def bounds(tile, a, b):
+            nc.vector.tensor_tensor(high[:, tile, :], a[:], b[:], MAX)
+            nc.vector.tensor_tensor(low[:, tile, :], a[:], b[:], MIN)
 
-        def bounds(got, tiles, vs):
-            nc.vector.tensor_tensor(high[:, tiles, vs], got[0][:], got[1][:], MAX)
-            nc.vector.tensor_tensor(low[:, tiles, vs], got[0][:], got[1][:], MIN)
-
-        def cap(got, tiles, vs):
-            nc.vector.tensor_tensor(capped[:, tiles, vs], high[:, tiles, vs], got[2][:], MIN)
+        def cap(tiles, vs, c):
+            nc.vector.tensor_tensor(capped[:, tiles, vs], high[:, tiles, vs], c[:], MIN)
 
         def close_mixed(h):
             nc.vector.tensor_tensor(mixed[h][:], low[:, h, :], capped[:, h, :], MAX)
-            for rows in (regrouped, out_rows):
-                for t in range(PAIR):
-                    nc.sync.dma_start(
-                        out=rows[h * HALF_P : (h + 1) * HALF_P, t, :], in_=mixed[h][t * HALF_P : (t + 1) * HALF_P, :]
-                    )
+            for t in range(PAIR):
+                nc.sync.dma_start(
+                    out=medians[h * HALF_P : (h + 1) * HALF_P, t, :], in_=mixed[h][t * HALF_P : (t + 1) * HALF_P, :]
+                )
 
         def close_straight(vs):
-            nc.vector.tensor_tensor(straight[:, :, vs], low[:, high_pair, vs], capped[:, high_pair, vs], MAX)
-            nc.sync.dma_start(out=out_rows[:, high_pair, vs], in_=straight[:, :, vs])
+            nc.vector.tensor_tensor(medians[:, high_pair, vs], low[:, high_pair, vs], capped[:, high_pair, vs], MAX)
+            nc.sync.dma_start(out=out_rows[:, high_pair, vs], in_=medians[:, high_pair, vs])
 
-        tile0, tile1 = slice(0, 1), slice(1, PAIR)
-        got0 = neighbours("got0_", tile0, whole, ("a0", "a1", "a2"))
-        got1 = neighbours("got1_", tile1, whole, ("b0", "b1", "a0"))
-        got_front = neighbours("got_front", high_pair, front, ("c0", "c1", "b1"))
-        got_back = neighbours("got_back", high_pair, back, ("d0", "d1", "d2"))
-        for i in range(2):
-            fetch(scalar_lookup, got0, i, 0, 0, whole)
-        fetch(vector_lookup, got0, 2, 0, 0, whole)
+        a0, b0 = [fetch(scalar_lookup, i, 0, "ab0_%d" % i) for i in range(2)]
+        c0 = fetch(vector_lookup, 2, 0, "c0")
         for tile in (1, 2):
             nc.vector.tensor_copy(out=y[tile][:], in_=banks[tile][:])
-        for i in range(2):
-            fetch(scalar_lookup, got1, i, 0, 1, whole)
+        a1, b1 = [fetch(scalar_lookup, i, 1, "ab1_%d" % i) for i in range(2)]
         nc.scalar.copy(out=y[3][:], in_=banks[3][:])
-        bounds(got0, tile0, whole)
-        cap(got0, tile0, whole)
-        fetch(vector_lookup, got1, 2, 0, 1, whole)
+        bounds(0, a0, b0)
+        cap(0, whole, c0)
+        c1 = fetch(vector_lookup, 2, 1, "ab0_0")
         close_mixed(0)
-        bounds(got1, tile1, whole)
-        cap(got1, tile1, whole)
-        fetch(vector_lookup, got_front, 2, 0, 2, front)
+        bounds(1, a1, b1)
+        cap(1, whole, c1)
+        ab = {tile: [fetch(scalar_lookup, i, tile, "ab%d_%d" % (tile, i)) for i in range(2)] for tile in (2, 3)}
+        c2 = fetch(scalar_lookup, 2, 2, "c2")
+        c3 = [sb.tile([P, HALF_V], F32, name="c3_%d" % i, tag=tag) for i, tag in enumerate(("ab1_1", "c3_back"))]
+        scalar_lookup(c3[1][:], y[3][:].indirect(entries(places[2], back)))
+        nc.vector.tensor_tensor(high[:, 2, :], ab[2][0][:], ab[2][1][:], MAX)
         close_mixed(1)
-        fetch(vector_lookup, got_front, 2, 1, 3, front)
-        for got, vs, count in ((got_front, front, 2), (got_back, back, 3)):
-            for i in range(count):
-                for slot in range(PAIR):
-                    fetch(scalar_lookup, got, i, slot, PAIR + slot, vs)
-        for got, vs in ((got_front, front), (got_back, back)):
-            bounds(got, high_pair, vs)
-            cap(got, high_pair, vs)
+        nc.sync.dma_start(out=out_rows[:, low_pair, :], in_=medians[:, low_pair, :])
+        nc.vector.tensor_tensor(low[:, 2, :], ab[2][0][:], ab[2][1][:], MIN)
+        vector_lookup(c3[0][:], y[3][:].indirect(entries(places[2], front)))
+        bounds(3, *ab[3])
+        cap(3, front, c3[0])
+        cap(2, whole, c2)
+        cap(3, back, c3[1])
         close_straight(front)
-        weave(nc.scalar.copy, o_bf[:, front, high_pair], straight[:, :, front])
-        weave(nc.scalar.copy, o_bf[:, front, low_pair], regrouped[:, :, front])
-        nc.vector.tensor_tensor(
-            by_runs_woven(o_bf[:, back, high_pair]),
-            by_runs_apart(low[:, high_pair, back]),
-            by_runs_apart(capped[:, high_pair, back]),
-            MAX,
-        )
+        weave(nc.scalar.copy, o_bf[:, front, :], medians[:, :, front])
         close_straight(back)
-        weave(nc.vector.tensor_copy, o_bf[:, back, low_pair], regrouped[:, :, back])
-        for vs in (back, front):
+        weave(nc.vector.tensor_copy, o_bf[:, back, :], medians[:, :, back])
+        for vs in (front, back):
             quantize(o_codes[:, vs], o_scales[:, vs], values_of(o_flat, vs))
         nc.sync.dma_start(out=out_words, in_=o_codes[:].bitcast(I32))
 

@@ -45,6 +45,7 @@ def tile_picked_median_none_lo_kernel(
         out_scales = out_2[0].bitcast(I32)
         low_pair, high_pair = slice(0, PAIR), slice(PAIR, PACK)
         first_half, second_half = slice(0, HALF_S), slice(HALF_S, S)
+        third_quarter, last_quarter = slice(HALF_S, S - P), slice(S - P, S)
 
         x_raw = [sb.tile([P, T], F32, name="x_raw%d" % j, align_bytes=LONG_ROW) for j in range(PACK)]
         w_first = sb.tile([P, 1, HALF_N], F32, name="w_first", align_bytes=LONG_ROW)
@@ -84,11 +85,11 @@ def tile_picked_median_none_lo_kernel(
         def quantize(words, scale_bytes, values):
             nc.vector.quantize_mx(out=words.bitcast(FP8X4), scales=scale_bytes, in_=values)
 
-        x_picked = sb.tile([P, PACK, HALF_S], BF16, name="x_picked")
+        x_picked = sb.tile([P, PACK, S], BF16, name="x_picked")
         rounded = sb.tile([P, (S + N) * PACK], BF16, name="rounded", align_bytes=64)
         codes = sb.tile([P, S + N], U32, name="codes", align_bytes=64)
         scales = sb.tile([P, S + N], U8, name="scales", align_bytes=64)
-        w_cols = [slice(S + tile * P, S + (tile + 1) * P) for tile in range(PACK)]
+        w_cols = [slice(S + slot * P, S + (slot + 1) * P) for slot in (0, 3, 1, 2)]
         straight_cols = slice(w_cols[2].start, w_cols[3].stop)
 
         def values_of(flat, cols):
@@ -115,18 +116,23 @@ def tile_picked_median_none_lo_kernel(
                 in_=w_raw[:].rearrange("p j (m t) -> p m j t", t=PACK)[:, :, :, high_pair],
             )
 
+        def weave_picked(engine_copy, js, cols):
+            weave(engine_copy, x_woven[:, cols, js], x_picked[:, js, cols])
+
         deal_mixed(nc.scalar.copy, 0, slice(0, 1), w_first)
         deal_straight(nc.scalar.copy, 0, slice(0, 1), w_first)
         for j in range(PACK):
-            vector_lookup(x_picked[:, j, :], x_raw[j][:].indirect(entries(picked, second_half)))
-            scalar_lookup(x_woven[:, first_half, j], x_raw[j][:].indirect(entries(picked, first_half)))
+            vector_lookup(x_picked[:, j, first_half], x_raw[j][:].indirect(entries(picked, first_half)))
+            scalar_lookup(x_picked[:, j, second_half], x_raw[j][:].indirect(entries(picked, second_half)))
             if j % PAIR == PAIR - 1:
                 js = slice(j + 1 - PAIR, j + 1)
-                weave(nc.vector.tensor_copy, x_woven[:, second_half, js], x_picked[:, js, :])
+                weave_picked(nc.vector.tensor_copy, js, first_half)
+                weave_picked(nc.vector.tensor_copy, js, third_quarter)
+                weave_picked(nc.scalar.copy, js, last_quarter)
         quantize_operands(first_half)
         deal_mixed(nc.scalar.copy, 0, slice(1, PACK), w_rest)
-        quantize_operands(w_cols[0])
-        quantize_operands(second_half)
+        quantize_operands(third_quarter)
+        quantize_operands(slice(last_quarter.start, w_cols[0].stop))
         deal_straight(nc.scalar.copy, 0, slice(1, PACK), w_rest)
         deal_mixed(nc.vector.tensor_copy, 1, slice(0, PACK), w_last)
         deal_straight(nc.scalar.copy, 1, slice(0, PACK), w_last)
@@ -148,10 +154,10 @@ def tile_picked_median_none_lo_kernel(
             )
             return acc
 
-        halves = (first_half, second_half)
-        first_banks = [product(0, cols) for cols in halves]
+        pieces = (first_half, third_quarter, last_quarter)
+        first_banks = [product(0, cols) for cols in pieces]
         banks = {1: product(1, slice(0, S))}
-        for bank, cols, engine_copy in zip(first_banks, halves, (nc.scalar.copy, nc.vector.tensor_copy)):
+        for bank, cols, engine_copy in zip(first_banks, pieces, (nc.vector.tensor_copy, nc.scalar.copy, nc.scalar.copy)):
             engine_copy(out=y[0][:, cols], in_=bank[:])
         quantize_operands(straight_cols)
         for tile in range(PAIR, PACK):

@@ -186,11 +186,15 @@ def tile_picked_median_none_lo_kernel(
         def cap(tiles, vs, c):
             nc.vector.tensor_tensor(capped[:, tiles, vs], high[:, tiles, vs], c[:], MIN)
 
+        def regroup(move, h):
+            for t in range(PAIR):
+                move(out=medians[h * HALF_P : (h + 1) * HALF_P, t, :], in_=mixed[h][t * HALF_P : (t + 1) * HALF_P, :])
+
         def close_mixed(h):
             nc.vector.tensor_tensor(mixed[h][:], low[:, h, :], capped[:, h, :], MAX)
             for t in range(PAIR):
                 nc.sync.dma_start(
-                    out=medians[h * HALF_P : (h + 1) * HALF_P, t, :], in_=mixed[h][t * HALF_P : (t + 1) * HALF_P, :]
+                    out=out_rows[h * HALF_P : (h + 1) * HALF_P, t, :], in_=mixed[h][t * HALF_P : (t + 1) * HALF_P, :]
                 )
 
         def close_straight(vs):
@@ -207,6 +211,7 @@ def tile_picked_median_none_lo_kernel(
         cap(0, whole, c0)
         c1 = fetch(vector_lookup, 2, 1, "ab0_0")
         close_mixed(0)
+        regroup(nc.sync.dma_start, 0)
         bounds(1, a1, b1)
         cap(1, whole, c1)
         ab = {tile: [fetch(scalar_lookup, i, tile, "ab%d_%d" % (tile, i)) for i in range(2)] for tile in (2, 3)}
@@ -215,7 +220,7 @@ def tile_picked_median_none_lo_kernel(
         scalar_lookup(c3[1][:], y[3][:].indirect(entries(places[2], back)))
         nc.vector.tensor_tensor(high[:, 2, :], ab[2][0][:], ab[2][1][:], MAX)
         close_mixed(1)
-        nc.sync.dma_start(out=out_rows[:, low_pair, :], in_=medians[:, low_pair, :])
+        regroup(nc.scalar.copy, 1)
         nc.vector.tensor_tensor(low[:, 2, :], ab[2][0][:], ab[2][1][:], MIN)
         vector_lookup(c3[0][:], y[3][:].indirect(entries(places[2], front)))
         bounds(3, *ab[3])

@@ -28,6 +28,7 @@ HALF_N = N // 2
 HALF_P = P // 2
 HALF_S = S // 2
 HALF_V = V // 2
+SCALAR_WEAVES = 64
 
 
 def tile_picked_median_none_lo_kernel(
@@ -192,6 +193,8 @@ def tile_picked_median_none_lo_kernel(
 
         def close_mixed(h):
             nc.vector.tensor_tensor(mixed[h][:], low[:, h, :], capped[:, h, :], MAX)
+
+        def store_mixed(h):
             for t in range(PAIR):
                 nc.sync.dma_start(
                     out=out_rows[h * HALF_P : (h + 1) * HALF_P, t, :], in_=mixed[h][t * HALF_P : (t + 1) * HALF_P, :]
@@ -212,25 +215,28 @@ def tile_picked_median_none_lo_kernel(
         c1 = fetch(vector_lookup, 2, 1, "ab0_0")
         close_mixed(0)
         regroup(nc.sync.dma_start, 0)
+        store_mixed(0)
         bounds(1, a1, b1)
         cap(1, whole, c1)
         ab = {tile: [fetch(scalar_lookup, i, tile, "ab%d_%d" % (tile, i)) for i in range(2)] for tile in (2, 3)}
-        c2 = fetch(scalar_lookup, 2, 2, "c2")
-        c3 = [sb.tile([P, HALF_V], F32, name="c3_%d" % i, tag=tag) for i, tag in enumerate(("ab1_1", "c3_back"))]
-        scalar_lookup(c3[1][:], y[3][:].indirect(entries(places[2], back)))
+        third = sb.tile([P, PAIR, V], F32, name="third")
+        scalar_lookup(third[:, 0, :], y[2][:].indirect(places[2][:]))
+        scalar_lookup(third[:, 1, back], y[3][:].indirect(entries(places[2], back)))
         nc.vector.tensor_tensor(high[:, 2, :], ab[2][0][:], ab[2][1][:], MAX)
         close_mixed(1)
+        store_mixed(1)
         regroup(nc.scalar.copy, 1)
         nc.vector.tensor_tensor(low[:, 2, :], ab[2][0][:], ab[2][1][:], MIN)
-        vector_lookup(c3[0][:], y[3][:].indirect(entries(places[2], front)))
+        vector_lookup(third[:, 1, front], y[3][:].indirect(entries(places[2], front)))
         bounds(3, *ab[3])
-        cap(3, front, c3[0])
-        cap(2, whole, c2)
-        cap(3, back, c3[1])
+        for vs in (front, back):
+            nc.vector.tensor_tensor(capped[:, high_pair, vs], high[:, high_pair, vs], third[:, :, vs], MIN)
         close_straight(front)
-        weave(nc.scalar.copy, o_bf[:, front, :], medians[:, :, front])
+        scalar_share = slice(0, SCALAR_WEAVES)
+        weave(nc.scalar.copy, o_bf[:, scalar_share, :], medians[:, :, scalar_share])
         close_straight(back)
-        weave(nc.vector.tensor_copy, o_bf[:, back, :], medians[:, :, back])
+        for vs in (slice(SCALAR_WEAVES, HALF_V), back):
+            weave(nc.vector.tensor_copy, o_bf[:, vs, :], medians[:, :, vs])
         for vs in (front, back):
             quantize(o_codes[:, vs], o_scales[:, vs], values_of(o_flat, vs))
         nc.sync.dma_start(out=out_words, in_=o_codes[:].bitcast(I32))

from contextlib import ExitStack

import concourse.mybir as mybir

K, T, S, V, N = 512, 1024, 512, 256, 512
FLOPS = 2 * K * N * S

F32 = mybir.dt.float32
BF16 = mybir.dt.bfloat16
I32 = mybir.dt.int32
U32 = mybir.dt.uint32
U16 = mybir.dt.uint16
U8 = mybir.dt.uint8
FP8X4 = mybir.dt.float8_e4m3fn_x4
MAX = mybir.AluOpType.max
MIN = mybir.AluOpType.min
COPY = mybir.ActivationFunctionType.Copy

P = 128
PACK = 4
PAIR = 2
LIST = 16
RUN = 4
QUADRANT = 32
SCALE_ROWS = 4
LONG_ROW = 256
HALF_N = N // 2
HALF_P = P // 2
HALF_S = S // 2
HALF_V = V // 2
SCALAR_WEAVES = 64


def tile_picked_median_none_lo_kernel(
    tc, xT, w1, offs, pos1, pos2, pos3, out_0, out_1, out_2
):
    nc = tc.nc
    with ExitStack() as ctx:
        sb = ctx.enter_context(tc.tile_pool(name="sb", bufs=1))
        ps = ctx.enter_context(tc.psum_pool(name="ps", bufs=1))

        x_rows = xT.rearrange("(p j) c -> p j c", j=PACK)
        w_rows = w1.rearrange("(p j) c -> p j c", j=PACK)
        out_rows = out_0.rearrange("(p t) v -> p t v", t=PACK)
        out_words = out_1[0].rearrange("p c r -> p (c r)").bitcast(I32)
        out_scales = out_2[0].bitcast(I32)
        low_pair, high_pair = slice(0, PAIR), slice(PAIR, PACK)
        first_half, second_half = slice(0, HALF_S), slice(HALF_S, S)
        third_quarter, last_quarter = slice(HALF_S, S - P), slice(S - P, S)

        x_raw = [sb.tile([P, T], F32, name="x_raw%d" % j, align_bytes=LONG_ROW) for j in range(PACK)]
        w_first = sb.tile([P, 1, HALF_N], F32, name="w_first", align_bytes=LONG_ROW)
        w_rest = sb.tile([P, PACK - 1, HALF_N], F32, name="w_rest", align_bytes=LONG_ROW)
        w_last = sb.tile([P, PACK, HALF_N], F32, name="w_last", tag="w_last", align_bytes=LONG_ROW)
        picked = sb.tile([P, S // LIST], U16, name="picked")
        nc.sync.dma_start(out=w_first[:], in_=w_rows[:, 0:1, 0:HALF_N])
        nc.sync.dma_start(picked[:], offs)
        for j in range(PACK):
            nc.sync.dma_start(out=x_raw[j][:], in_=x_rows[:, j, :])
        nc.sync.dma_start(out=w_rest[:], in_=w_rows[:, 1:PACK, 0:HALF_N])
        nc.sync.dma_start(out=w_last[:], in_=w_rows[:, :, HALF_N:N])
        places = []
        for i, pos in enumerate((pos1, pos2, pos3)):
            place = sb.tile([P, V // LIST], U16, name="place%d" % i)
            nc.sync.dma_start(place[:], pos)
            places.append(place)

        def vector_lookup(dst, src):
            nc.vector.tensor_copy(dst, src)

        def scalar_lookup(dst, src):
            nc.scalar.activation(dst, src, COPY)

        def entries(list_tile, span):
            return list_tile[:, span.start // LIST : span.stop // LIST]

        def by_runs_woven(ap):
            return ap.rearrange("p (c i) e -> p c e i", i=RUN)

        def by_runs_apart(ap):
            return ap.rearrange("p e (c i) -> p c e i", i=RUN)

        def weave(engine_copy, dst, src):
            engine_copy(out=by_runs_woven(dst), in_=by_runs_apart(src))

        def quantize(words, scale_bytes, values):
            nc.vector.quantize_mx(out=words.bitcast(FP8X4), scales=scale_bytes, in_=values)

        x_picked = sb.tile([P, PACK, S], BF16, name="x_picked")
        rounded = sb.tile([P, (S + N) * PACK], BF16, name="rounded", align_bytes=64)
        codes = sb.tile([P, S + N], U32, name="codes", align_bytes=64)
        scales = sb.tile([P, S + N], U8, name="scales", align_bytes=64)
        w_cols = [slice(S + slot * P, S + (slot + 1) * P) for slot in (0, 3, 1, 2)]
        straight_cols = slice(w_cols[2].start, w_cols[3].stop)

        def values_of(flat, cols):
            return flat[:, cols.start * PACK : cols.stop * PACK]

        def quantize_operands(cols):
            quantize(codes[:, cols], scales[:, cols], values_of(rounded, cols))

        x_woven = values_of(rounded, slice(0, S)).rearrange("p (s j) -> p s j", j=PACK)
        mixed_dealt = [
            values_of(rounded, w_cols[h]).rearrange("p (t m j) -> p m j t", t=PAIR, j=PACK) for h in range(PAIR)
        ]
        straight_dealt = values_of(rounded, straight_cols).rearrange("p (t h m j) -> p h m j t", t=PAIR, h=PAIR, j=PACK)

        def deal_mixed(engine_copy, h, js, w_raw):
            engine_copy(
                out=mixed_dealt[h][:, :, js, :],
                in_=w_raw[:].rearrange("p j (m t) -> p m j t", t=PACK)[:, :, :, low_pair],
            )

        def deal_straight(engine_copy, h, js, w_raw):
            engine_copy(
                out=straight_dealt[:, h, :, js, :],
                in_=w_raw[:].rearrange("p j (m t) -> p m j t", t=PACK)[:, :, :, high_pair],
            )

        def weave_picked(engine_copy, js, cols):
            weave(engine_copy, x_woven[:, cols, js], x_picked[:, js, cols])

        deal_mixed(nc.scalar.copy, 0, slice(0, 1), w_first)
        deal_straight(nc.scalar.copy, 0, slice(0, 1), w_first)
        for j in range(PACK):
            vector_lookup(x_picked[:, j, first_half], x_raw[j][:].indirect(entries(picked, first_half)))
            scalar_lookup(x_picked[:, j, second_half], x_raw[j][:].indirect(entries(picked, second_half)))
            if j % PAIR == PAIR - 1:
                js = slice(j + 1 - PAIR, j + 1)
                weave_picked(nc.vector.tensor_copy, js, first_half)
                weave_picked(nc.vector.tensor_copy, js, third_quarter)
                weave_picked(nc.scalar.copy, js, last_quarter)
        quantize_operands(first_half)
        deal_mixed(nc.scalar.copy, 0, slice(1, PACK), w_rest)
        quantize_operands(third_quarter)
        quantize_operands(slice(last_quarter.start, w_cols[0].stop))
        deal_straight(nc.scalar.copy, 0, slice(1, PACK), w_rest)
        deal_mixed(nc.vector.tensor_copy, 1, slice(0, PACK), w_last)
        deal_straight(nc.scalar.copy, 1, slice(0, PACK), w_last)
        quantize_operands(w_cols[1])

        y = [sb.tile([P, S], F32, name="y0", tag="w_last", align_bytes=LONG_ROW)]
        y.extend(sb.tile([P, S], F32, name="y%d" % tile) for tile in range(1, PACK))

        def product(tile, cols):
            acc = ps.tile([P, cols.stop - cols.start], F32, name="acc%d_%d" % (tile, cols.start))
            nc.tensor.matmul_mx(
                out=acc[:],
                lhsT=codes[:, w_cols[tile]].bitcast(FP8X4),
                lhsT_scale=scales[:, w_cols[tile]],
                rhs=codes[:, cols].bitcast(FP8X4),
                rhs_scale=scales[:, cols],
                start=True,
                stop=True,
            )
            return acc

        pieces = (first_half, third_quarter, last_quarter)
        first_banks = [product(0, cols) for cols in pieces]
        banks = {1: product(1, slice(0, S))}
        for bank, cols, engine_copy in zip(first_banks, pieces, (nc.vector.tensor_copy, nc.scalar.copy, nc.scalar.copy)):
            engine_copy(out=y[0][:, cols], in_=bank[:])
        quantize_operands(straight_cols)
        for tile in range(PAIR, PACK):
            banks[tile] = product(tile, slice(0, S))

        high = sb.tile([P, PACK, V], F32, name="high")
        low = sb.tile([P, PACK, V], F32, name="low")
        capped = sb.tile([P, PACK, V], F32, name="capped")
        mixed = [sb.tile([P, V], F32, name="mixed%d" % h) for h in range(PAIR)]
        medians = sb.tile([P, PACK, V], F32, name="medians")
        o_bf = sb.tile([P, V, PACK], BF16, name="o_bf", align_bytes=64)
        o_codes = sb.tile([P, V], U32, name="o_codes", align_bytes=64)
        o_scales = sb.tile([P, V], U8, name="o_scales", align_bytes=64)
        o_flat = o_bf[:].rearrange("p v t -> p (v t)")
        whole, front, back = slice(0, V), slice(0, HALF_V), slice(HALF_V, V)

        def fetch(lookup, i, tile, buffer):
            got = sb.tile([P, V], F32, name="got%d_%d" % (tile, i), tag=buffer)
            lookup(got[:], y[tile][:].indirect(places[i][:]))
            return got

        def bounds(tile, a, b):
            nc.vector.tensor_tensor(high[:, tile, :], a[:], b[:], MAX)
            nc.vector.tensor_tensor(low[:, tile, :], a[:], b[:], MIN)

        def cap(tiles, vs, c):
            nc.vector.tensor_tensor(capped[:, tiles, vs], high[:, tiles, vs], c[:], MIN)

        def regroup(move, h):
            for t in range(PAIR):
                move(out=medians[h * HALF_P : (h + 1) * HALF_P, t, :], in_=mixed[h][t * HALF_P : (t + 1) * HALF_P, :])

        def close_mixed(h):
            nc.vector.tensor_tensor(mixed[h][:], low[:, h, :], capped[:, h, :], MAX)

        def store_mixed(h):
            for t in range(PAIR):
                nc.sync.dma_start(
                    out=out_rows[h * HALF_P : (h + 1) * HALF_P, t, :], in_=mixed[h][t * HALF_P : (t + 1) * HALF_P, :]
                )

        def close_straight(vs):
            nc.vector.tensor_tensor(medians[:, high_pair, vs], low[:, high_pair, vs], capped[:, high_pair, vs], MAX)
            nc.sync.dma_start(out=out_rows[:, high_pair, vs], in_=medians[:, high_pair, vs])

        a0, b0 = [fetch(scalar_lookup, i, 0, "ab0_%d" % i) for i in range(2)]
        c0 = fetch(vector_lookup, 2, 0, "c0")
        for tile in (1, 2):
            nc.vector.tensor_copy(out=y[tile][:], in_=banks[tile][:])
        a1, b1 = [fetch(scalar_lookup, i, 1, "ab1_%d" % i) for i in range(2)]
        nc.scalar.copy(out=y[3][:], in_=banks[3][:])
        bounds(0, a0, b0)
        cap(0, whole, c0)
        c1 = fetch(vector_lookup, 2, 1, "ab0_0")
        close_mixed(0)
        regroup(nc.sync.dma_start, 0)
        store_mixed(0)
        bounds(1, a1, b1)
        cap(1, whole, c1)
        ab = {tile: [fetch(scalar_lookup, i, tile, "ab%d_%d" % (tile, i)) for i in range(2)] for tile in (2, 3)}
        third = sb.tile([P, PAIR, V], F32, name="third")
        scalar_lookup(third[:, 0, :], y[2][:].indirect(places[2][:]))
        scalar_lookup(third[:, 1, back], y[3][:].indirect(entries(places[2], back)))
        nc.vector.tensor_tensor(high[:, 2, :], ab[2][0][:], ab[2][1][:], MAX)
        close_mixed(1)
        store_mixed(1)
        regroup(nc.scalar.copy, 1)
        nc.vector.tensor_tensor(low[:, 2, :], ab[2][0][:], ab[2][1][:], MIN)
        vector_lookup(third[:, 1, front], y[3][:].indirect(entries(places[2], front)))
        bounds(3, *ab[3])
        for vs in (front, back):
            nc.vector.tensor_tensor(capped[:, high_pair, vs], high[:, high_pair, vs], third[:, :, vs], MIN)
        close_straight(front)
        scalar_share = slice(0, SCALAR_WEAVES)
        weave(nc.scalar.copy, o_bf[:, scalar_share, :], medians[:, :, scalar_share])
        close_straight(back)
        for vs in (slice(SCALAR_WEAVES, HALF_V), back):
            weave(nc.vector.tensor_copy, o_bf[:, vs, :], medians[:, :, vs])
        for vs in (front, back):
            quantize(o_codes[:, vs], o_scales[:, vs], values_of(o_flat, vs))
        nc.sync.dma_start(out=out_words, in_=o_codes[:].bitcast(I32))

        scale_rows = o_scales[:].bitcast(I32)
        for q in range(P // QUADRANT):
            queue = nc.sync if q % 2 == 0 else nc.scalar
            queue.dma_start(
                out=out_scales[SCALE_ROWS * q : SCALE_ROWS * (q + 1), :],
                in_=scale_rows[QUADRANT * q : QUADRANT * q + SCALE_ROWS, :],
            )
